import numpy as np
import ml_dtypes


def mxq(x, axis, fmt="e4m3"):
    dtype, down = {"e4m3": (ml_dtypes.float8_e4m3fn, 7), "e5m2": (ml_dtypes.float8_e5m2, 14)}[fmt]
    v = np.moveaxis(np.asarray(x, np.float32).astype(ml_dtypes.bfloat16).astype(np.float64), axis, -1)
    blocks = v.reshape(v.shape[:-1] + (-1, 32))
    amax = np.abs(blocks).max(-1, keepdims=True)
    byte = np.maximum(np.where(amax > 0, np.frexp(amax)[1] - 1 + 127, 0) - down, 1)
    scale = np.exp2(byte - 127.0)
    codes = (blocks / scale).astype(np.float32).astype(dtype).astype(np.float64)
    return np.moveaxis((codes * scale).reshape(v.shape), -1, axis)


WIDE = False


def mx_kscale(k):
    if not WIDE:
        return np.ones(k)
    levels = np.array([10, -10, 5, -5, 0])
    if k % 512:
        return np.exp2(np.random.permutation(np.resize(levels, k // 32))).repeat(32)
    a = np.empty((k // 512, 16))
    for p in range(k // 512):
        a[p, :8] = np.random.permutation(np.resize(levels, 8))
        for g in range(8):
            far = levels[np.abs(levels - a[p, g]) >= 10]
            a[p, g + 8] = far[np.random.randint(len(far))]
    return np.exp2(a.ravel()).repeat(32)


def f64(x):
    return np.asarray(x).astype(np.float64)


def striped(idx):
    return np.tile(idx.reshape(-1, 16).T, (8, 1)).astype(np.uint16)


def unstriped(offs):
    return offs[:16].T.reshape(-1).astype(np.int64)


E2M1 = np.array([0.0, 0.5, 1.0, 1.5, 2.0, 3.0, 4.0, 6.0, -0.0, -0.5, -1.0, -1.5, -2.0, -3.0, -4.0, -6.0])


def pack_weight(w, fmt):
    k, n = w.shape
    w = f64(np.asarray(w, np.float32).astype(ml_dtypes.bfloat16)).reshape(k // 32, 32, n)
    amax = np.abs(w).max(1)
    if fmt == "e4m3":
        byte = np.frexp(amax)[1] - 1 + 127 - 7
    else:
        mant, ex = np.frexp(amax / 6.0)
        byte = np.where(mant > 0.5, ex, ex - 1) + 127
    byte = np.clip(np.where(amax > 0, byte, 1), 1, 254)
    scaled = (w * np.exp2(127.0 - byte)[:, None, :]).reshape(k, n).astype(np.float32)
    by_word = np.ascontiguousarray(scaled.reshape(k // 512, 128, 4, n).transpose(0, 1, 3, 2))
    if fmt == "e4m3":
        words = by_word.astype(ml_dtypes.float8_e4m3fn).view(np.uint8)
    else:
        c = by_word.astype(ml_dtypes.float4_e2m1fn).view(np.uint8) & 0xF
        words = (c[..., 0::2] | (c[..., 1::2] << 4)).reshape(k // 512, 128, 2 * n)
    return np.ascontiguousarray(words), np.ascontiguousarray(byte.astype(np.uint8).reshape(k // 512, 16, n))


def unpack_weight(words, scales, fmt):
    g, _, n = scales.shape
    words = np.ascontiguousarray(words).reshape(g, 128, n, -1)
    if fmt == "e4m3":
        vals = words.view(ml_dtypes.float8_e4m3fn).astype(np.float64)
    else:
        nib = np.empty((g, 128, n, 4), np.uint8)
        nib[..., 0::2] = words & 0xF
        nib[..., 1::2] = words >> 4
        vals = E2M1[nib]
    vals = vals * np.repeat(np.exp2(scales.astype(np.float64) - 127.0), 8, axis=1)[..., None]
    return vals.transpose(0, 1, 3, 2).reshape(g * 512, n)


def relu2(v):
    return np.maximum(v, 0.0) ** 2


K, T, E, C, N = 1024, 1024, 8, 256, 512


def by_slot(wq, xq):
    return np.concatenate([xq[:, e * C:(e + 1) * C].T @ wq[e] for e in range(E)])


def setup_inputs():
    n = np.random.standard_normal
    s = mx_kscale(K)
    slot_token = np.concatenate([np.random.permutation(T)[:C] for e in range(E)])
    x = pack_weight(n((K, T)) * s[:, None], "e2m1")
    two = np.ascontiguousarray(x[0].reshape(K // 1024, 2, 128, T, 2).transpose(0, 2, 3, 1, 4).reshape(K // 1024, 128, T, 4))
    return {
        "x_words": two,
        "x_scales": x[1],
        "w": (n((E, K, N)) / np.sqrt(K) / s[None, :, None]).astype(np.float32),
        "offs": striped(slot_token),
    }


def reference(x_words, x_scales, w, offs):
    wq = mxq(f64(w), 1, "e4m3")
    idx = unstriped(offs)
    words = x_words.reshape(K // 1024, 128, T, 2, 2).transpose(0, 3, 1, 2, 4).reshape(K // 512, 128, 2 * T)
    xq = unpack_weight(words, x_scales, "e2m1")[:, idx]
    y = relu2(by_slot(wq, xq))
    return y

@@ -1,0 +1,140 @@
+from contextlib import ExitStack
+
+import concourse.mybir as mybir
+
+K, T, E, C, N = 1024, 1024, 8, 256, 512
+FLOPS = 2 * E * C * K * N
+
+F32 = mybir.dt.float32
+BF16 = mybir.dt.bfloat16
+I32 = mybir.dt.int32
+U32 = mybir.dt.uint32
+U16 = mybir.dt.uint16
+U8 = mybir.dt.uint8
+FP8X4 = mybir.dt.float8_e4m3fn_x4
+FP4X4 = mybir.dt.float4_e2m1fn_x4
+ACT = mybir.ActivationFunctionType
+
+P = 128
+PACK = 4
+K_PASS = P * PACK
+PASSES = K // K_PASS
+HALVES = C // P
+RUN = 4
+CUT = 512
+SCALAR_EXPERTS = 3
+RESULT_SLOT = (5, 0, 1, 2)
+
+
+def tile_moe_s_lin_relu2_kernel(tc, x_words, x_scales, w, offs, out):
+    nc = tc.nc
+    with ExitStack() as ctx:
+        keep = ctx.enter_context(tc.tile_pool(name="keep", bufs=1))
+        big = ctx.enter_context(tc.tile_pool(name="big", bufs=1))
+        ring = ctx.enter_context(tc.tile_pool(name="ring", bufs=6))
+        rounded = ctx.enter_context(tc.tile_pool(name="rounded", bufs=10))
+        psum = ctx.enter_context(tc.psum_pool(name="psum", bufs=8))
+
+        offsets = keep.tile([P, E * C // 16], U16, name="offsets")
+        words = keep.tile([P, T], I32, name="words", align_bytes=64)
+        scales = keep.tile([P, T // 4], I32, name="scales", align_bytes=64)
+        both = keep.tile([P, E * C], U8, name="both", align_bytes=64)
+        second = keep.tile([P, E * C // 4], I32, name="second", align_bytes=64)
+
+        nc.vector.memset(scales[:], 0)
+        nc.vector.memset(second[:], 0)
+        for q in range(4):
+            nc.scalar.dma_start(
+                out=scales[32 * q:32 * q + 8, :], in_=x_scales[:, 4 * q:4 * q + 4, :].bitcast(I32)
+            )
+        nc.sync.dma_start(offsets[:], offs)
+        nc.sync.dma_start(out=words[:], in_=x_words[0].rearrange("p t d -> p (t d)").bitcast(I32))
+
+        raw = {}
+        for e in range(E):
+            for s in range(PASSES):
+                raw[e, s] = big.tile([P, PACK, N], F32, name="big%d" % (PASSES * e + s))
+                nc.sync.dma_start(
+                    out=raw[e, s][:],
+                    in_=w[e, s * K_PASS:(s + 1) * K_PASS, :].rearrange("(p j) n -> p j n", j=PACK),
+                )
+
+        for c in range(E * C // CUT):
+            slots = offsets[:, c * CUT // 16:(c + 1) * CUT // 16]
+            nc.vector.tensor_copy(out=both[:, c * CUT:(c + 1) * CUT], in_=scales[:].bitcast(U8).indirect(slots))
+        for q in range(4):
+            nc.gpsimd.dma_start(out=second[32 * q:32 * q + 4, :], in_=both[32 * q + 4:32 * q + 8, :].bitcast(I32))
+        x_scale = [both[:], second[:].bitcast(U8)]
+
+        paired = keep.tile([P, E * C], U32, name="paired", align_bytes=64)
+        x_code = keep.tile([P, PASSES, 2 * E * C], U8, name="x_code", align_bytes=64)
+        for c in range(E * C // CUT):
+            slots = offsets[:, c * CUT // 16:(c + 1) * CUT // 16]
+            nc.vector.tensor_copy(out=paired[:, c * CUT:(c + 1) * CUT], in_=words[:].bitcast(U32).indirect(slots))
+        for c in range(E * C // CUT):
+            nc.vector.tensor_copy(
+                out=x_code[:, :, 2 * c * CUT:2 * (c + 1) * CUT].bitcast(U16),
+                in_=paired[:, c * CUT:(c + 1) * CUT].bitcast(U16).rearrange("p (u s) -> p s u", s=PASSES),
+            )
+
+        for e in range(E):
+
+            grouped = []
+            for s in range(PASSES):
+                g = rounded.tile([P, N, PACK], BF16, name="grouped", align_bytes=64)
+                dst = g[:].rearrange("p (c i) t -> p c t i", i=RUN)
+                src = raw[e, s][:].rearrange("p t (c i) -> p c t i", i=RUN)
+                if e < SCALAR_EXPERTS:
+                    nc.scalar.activation(out=dst, in_=src, func=ACT.Copy)
+                else:
+                    nc.vector.tensor_copy(out=dst, in_=src)
+                grouped.append(g)
+            w_code = []
+            w_scale = []
+            for s in range(PASSES):
+                code = ring.tile([P, N], U32, name="w_code", align_bytes=64)
+                scale = ring.tile([P, N], U8, name="w_scale", align_bytes=64)
+                nc.vector.quantize_mx(
+                    out=code[:].bitcast(FP8X4),
+                    scales=scale[:],
+                    in_=grouped[s][:].rearrange("p n t -> p (n t)"),
+                )
+                w_code.append(code)
+                w_scale.append(scale)
+
+            acc = [psum.tile([P, N], F32, name="acc") for h in range(HALVES)]
+            for s in range(PASSES):
+                for h in range(HALVES):
+                    nc.tensor.matmul_mx(
+                        out=acc[h][:],
+                        lhsT=x_code[:, s, 2 * (C * e + P * h):2 * (C * e + P * (h + 1))].bitcast(FP4X4),
+                        lhsT_scale=x_scale[s][:, C * e + P * h:C * e + P * (h + 1)],
+                        rhs=w_code[s][:].bitcast(FP8X4),
+                        rhs_scale=w_scale[s][:],
+                        start=(s == 0),
+                        stop=(s == PASSES - 1),
+                    )
+            if e % 2 == 0:
+                y = big.tile([P, 2 * HALVES, N], F32, name="big%d" % RESULT_SLOT[e // 2])
+            first = (e % 2) * HALVES
+            if e == E - 1:
+                positive = keep.tile([P, N], F32, name="positive")
+                nc.scalar.activation(out=y[:, first, :], in_=acc[0][:], func=ACT.Relu)
+                nc.vector.tensor_scalar_max(positive[:], acc[1][:], 0.0)
+                nc.scalar.activation(out=y[:, first, :], in_=y[:, first, :], func=ACT.Square)
+                nc.vector.tensor_tensor(y[:, first + 1, :], acc[1][:], positive[:], mybir.AluOpType.mult)
+            else:
+                for h in range(HALVES):
+                    nc.scalar.activation(out=y[:, first + h, :], in_=acc[h][:], func=ACT.Relu)
+                for h in range(HALVES):
+                    nc.scalar.activation(out=y[:, first + h, :], in_=y[:, first + h, :], func=ACT.Square)
+            if e >= E - 2:
+                nc.sync.dma_start(
+                    out=out[e * C:(e + 1) * C, :].rearrange("(h p) n -> p h n", p=P),
+                    in_=y[:, first:first + HALVES, :],
+                )
+            elif e % 2 == 1:
+                nc.sync.dma_start(
+                    out=out[(e - 1) * C:(e + 1) * C, :].rearrange("(h p) n -> p h n", p=P),
+                    in_=y[:],
+                )

@@ -22,8 +22,9 @@ PASSES = K // K_PASS
 HALVES = C // P
 RUN = 4
 CUT = 512
-SCALAR_EXPERTS = 3
-RESULT_SLOT = (5, 0, 1, 2)
+PARK = 8
+SCALAR_EXPERTS = 4
+RESULT_SLOT = (7, 8, 0, 1)
 
 
 def tile_moe_s_lin_relu2_kernel(tc, x_words, x_scales, w, offs, out):
@@ -31,8 +32,8 @@ def tile_moe_s_lin_relu2_kernel(tc, x_words, x_scales, w, offs, out):
     with ExitStack() as ctx:
         keep = ctx.enter_context(tc.tile_pool(name="keep", bufs=1))
         big = ctx.enter_context(tc.tile_pool(name="big", bufs=1))
-        ring = ctx.enter_context(tc.tile_pool(name="ring", bufs=6))
-        rounded = ctx.enter_context(tc.tile_pool(name="rounded", bufs=10))
+        ring = ctx.enter_context(tc.tile_pool(name="ring", bufs=E * PASSES))
+        rounded = ctx.enter_context(tc.tile_pool(name="rounded", bufs=8))
         psum = ctx.enter_context(tc.psum_pool(name="psum", bufs=8))
 
         offsets = keep.tile([P, E * C // 16], U16, name="offsets")
@@ -44,9 +45,8 @@ def tile_moe_s_lin_relu2_kernel(tc, x_words, x_scales, w, offs, out):
         nc.vector.memset(scales[:], 0)
         nc.vector.memset(second[:], 0)
         for q in range(4):
-            nc.scalar.dma_start(
-                out=scales[32 * q:32 * q + 8, :], in_=x_scales[:, 4 * q:4 * q + 4, :].bitcast(I32)
-            )
+            nc.scalar.dma_start(out=scales[32 * q:32 * q + 4, :], in_=x_scales[0, 4 * q:4 * q + 4, :].bitcast(I32))
+        nc.scalar.dma_start(out=scales[PARK:PARK + 16, :], in_=x_scales[1].bitcast(I32))
         nc.sync.dma_start(offsets[:], offs)
         nc.sync.dma_start(out=words[:], in_=x_words[0].rearrange("p t d -> p (t d)").bitcast(I32))
 
@@ -63,7 +63,7 @@ def tile_moe_s_lin_relu2_kernel(tc, x_words, x_scales, w, offs, out):
             slots = offsets[:, c * CUT // 16:(c + 1) * CUT // 16]
             nc.vector.tensor_copy(out=both[:, c * CUT:(c + 1) * CUT], in_=scales[:].bitcast(U8).indirect(slots))
         for q in range(4):
-            nc.gpsimd.dma_start(out=second[32 * q:32 * q + 4, :], in_=both[32 * q + 4:32 * q + 8, :].bitcast(I32))
+            nc.gpsimd.dma_start(out=second[32 * q:32 * q + 4, :], in_=both[PARK + 4 * q:PARK + 4 * q + 4, :].bitcast(I32))
         x_scale = [both[:], second[:].bitcast(U8)]
 
         paired = keep.tile([P, E * C], U32, name="paired", align_bytes=64)
@@ -122,7 +122,7 @@ def tile_moe_s_lin_relu2_kernel(tc, x_words, x_scales, w, offs, out):
                 nc.scalar.activation(out=y[:, first, :], in_=acc[0][:], func=ACT.Relu)
                 nc.vector.tensor_scalar_max(positive[:], acc[1][:], 0.0)
                 nc.scalar.activation(out=y[:, first, :], in_=y[:, first, :], func=ACT.Square)
-                nc.vector.tensor_tensor(y[:, first + 1, :], acc[1][:], positive[:], mybir.AluOpType.mult)
+                nc.vector.tensor_tensor(y[:, first + 1, :], positive[:], positive[:], mybir.AluOpType.mult)
             else:
                 for h in range(HALVES):
                     nc.scalar.activation(out=y[:, first + h, :], in_=acc[h][:], func=ACT.Relu)

@@ -36,11 +36,11 @@ def tile_moe_s_lin_relu2_kernel(tc, x_words, x_scales, w, offs, out):
         rounded = ctx.enter_context(tc.tile_pool(name="rounded", bufs=8))
         psum = ctx.enter_context(tc.psum_pool(name="psum", bufs=8))
 
-        offsets = keep.tile([P, E * C // 16], U16, name="offsets")
-        words = keep.tile([P, T], I32, name="words", align_bytes=64)
-        scales = keep.tile([P, T // 4], I32, name="scales", align_bytes=64)
-        both = keep.tile([P, E * C], U8, name="both", align_bytes=64)
-        second = keep.tile([P, E * C // 4], I32, name="second", align_bytes=64)
+        offsets = keep.tile([P, E * C // 16], U16, name="offsets", align_bytes=256)
+        words = keep.tile([P, T], I32, name="words", align_bytes=256)
+        scales = keep.tile([P, T // 4], I32, name="scales", align_bytes=256)
+        both = keep.tile([P, E * C], U8, name="both", align_bytes=256)
+        second = keep.tile([P, E * C // 4], I32, name="second", align_bytes=256)
 
         nc.vector.memset(scales[:], 0)
         nc.vector.memset(second[:], 0)
@@ -53,7 +53,7 @@ def tile_moe_s_lin_relu2_kernel(tc, x_words, x_scales, w, offs, out):
         raw = {}
         for e in range(E):
             for s in range(PASSES):
-                raw[e, s] = big.tile([P, PACK, N], F32, name="big%d" % (PASSES * e + s))
+                raw[e, s] = big.tile([P, PACK, N], F32, name="big%d" % (PASSES * e + s), align_bytes=256)
                 nc.sync.dma_start(
                     out=raw[e, s][:],
                     in_=w[e, s * K_PASS:(s + 1) * K_PASS, :].rearrange("(p j) n -> p j n", j=PACK),
@@ -66,8 +66,8 @@ def tile_moe_s_lin_relu2_kernel(tc, x_words, x_scales, w, offs, out):
             nc.gpsimd.dma_start(out=second[32 * q:32 * q + 4, :], in_=both[PARK + 4 * q:PARK + 4 * q + 4, :].bitcast(I32))
         x_scale = [both[:], second[:].bitcast(U8)]
 
-        paired = keep.tile([P, E * C], U32, name="paired", align_bytes=64)
-        x_code = keep.tile([P, PASSES, 2 * E * C], U8, name="x_code", align_bytes=64)
+        paired = keep.tile([P, E * C], U32, name="paired", align_bytes=256)
+        x_code = keep.tile([P, PASSES, 2 * E * C], U8, name="x_code", align_bytes=256)
         for c in range(E * C // CUT):
             slots = offsets[:, c * CUT // 16:(c + 1) * CUT // 16]
             nc.vector.tensor_copy(out=paired[:, c * CUT:(c + 1) * CUT], in_=words[:].bitcast(U32).indirect(slots))
@@ -81,7 +81,7 @@ def tile_moe_s_lin_relu2_kernel(tc, x_words, x_scales, w, offs, out):
 
             grouped = []
             for s in range(PASSES):
-                g = rounded.tile([P, N, PACK], BF16, name="grouped", align_bytes=64)
+                g = rounded.tile([P, N, PACK], BF16, name="grouped", align_bytes=256)
                 dst = g[:].rearrange("p (c i) t -> p c t i", i=RUN)
                 src = raw[e, s][:].rearrange("p t (c i) -> p c t i", i=RUN)
                 if e < SCALAR_EXPERTS:
@@ -92,8 +92,8 @@ def tile_moe_s_lin_relu2_kernel(tc, x_words, x_scales, w, offs, out):
             w_code = []
             w_scale = []
             for s in range(PASSES):
-                code = ring.tile([P, N], U32, name="w_code", align_bytes=64)
-                scale = ring.tile([P, N], U8, name="w_scale", align_bytes=64)
+                code = ring.tile([P, N], U32, name="w_code", align_bytes=256)
+                scale = ring.tile([P, N], U8, name="w_scale", align_bytes=256)
                 nc.vector.quantize_mx(
                     out=code[:].bitcast(FP8X4),
                     scales=scale[:],
@@ -115,7 +115,7 @@ def tile_moe_s_lin_relu2_kernel(tc, x_words, x_scales, w, offs, out):
                         stop=(s == PASSES - 1),
                     )
             if e % 2 == 0:
-                y = big.tile([P, 2 * HALVES, N], F32, name="big%d" % RESULT_SLOT[e // 2])
+                y = big.tile([P, 2 * HALVES, N], F32, name="big%d" % RESULT_SLOT[e // 2], align_bytes=256)
             first = (e % 2) * HALVES
             if e == E - 1:
                 positive = keep.tile([P, N], F32, name="positive")

@@ -40,6 +40,7 @@ def tile_moe_s_lin_relu2_kernel(tc, x_words, x_scales, w, offs, out):
         words = keep.tile([P, T], I32, name="words", align_bytes=256)
         scales = keep.tile([P, T // 4], I32, name="scales", align_bytes=256)
         both = keep.tile([P, E * C], U8, name="both", align_bytes=256)
+        ordered = keep.tile([P, E * C], U8, name="ordered", align_bytes=256)
         second = keep.tile([P, E * C // 4], I32, name="second", align_bytes=256)
 
         nc.vector.memset(scales[:], 0)
@@ -62,9 +63,13 @@ def tile_moe_s_lin_relu2_kernel(tc, x_words, x_scales, w, offs, out):
         for c in range(E * C // CUT):
             slots = offsets[:, c * CUT // 16:(c + 1) * CUT // 16]
             nc.vector.tensor_copy(out=both[:, c * CUT:(c + 1) * CUT], in_=scales[:].bitcast(U8).indirect(slots))
+        nc.vector.tensor_copy(
+            out=ordered[:].rearrange("p (e h m) -> p e h m", e=E, h=HALVES),
+            in_=both[:].rearrange("p (e m h) -> p e h m", e=E, h=HALVES),
+        )
         for q in range(4):
-            nc.gpsimd.dma_start(out=second[32 * q:32 * q + 4, :], in_=both[PARK + 4 * q:PARK + 4 * q + 4, :].bitcast(I32))
-        x_scale = [both[:], second[:].bitcast(U8)]
+            nc.gpsimd.dma_start(out=second[32 * q:32 * q + 4, :], in_=ordered[PARK + 4 * q:PARK + 4 * q + 4, :].bitcast(I32))
+        x_scale = [ordered[:], second[:].bitcast(U8)]
 
         paired = keep.tile([P, E * C], U32, name="paired", align_bytes=256)
         x_code = keep.tile([P, PASSES, 2 * E * C], U8, name="x_code", align_bytes=256)
@@ -73,8 +78,8 @@ def tile_moe_s_lin_relu2_kernel(tc, x_words, x_scales, w, offs, out):
             nc.vector.tensor_copy(out=paired[:, c * CUT:(c + 1) * CUT], in_=words[:].bitcast(U32).indirect(slots))
         for c in range(E * C // CUT):
             nc.vector.tensor_copy(
-                out=x_code[:, :, 2 * c * CUT:2 * (c + 1) * CUT].bitcast(U16),
-                in_=paired[:, c * CUT:(c + 1) * CUT].bitcast(U16).rearrange("p (u s) -> p s u", s=PASSES),
+                out=x_code[:, :, 2 * c * CUT:2 * (c + 1) * CUT].bitcast(U16).rearrange("p s (e h m) -> p s e h m", h=HALVES, m=P),
+                in_=paired[:, c * CUT:(c + 1) * CUT].bitcast(U16).rearrange("p (e m h s) -> p s e h m", s=PASSES, h=HALVES, m=P),
             )
 
         for e in range(E):
@@ -130,11 +135,11 @@ def tile_moe_s_lin_relu2_kernel(tc, x_words, x_scales, w, offs, out):
                     nc.scalar.activation(out=y[:, first + h, :], in_=y[:, first + h, :], func=ACT.Square)
             if e >= E - 2:
                 nc.sync.dma_start(
-                    out=out[e * C:(e + 1) * C, :].rearrange("(h p) n -> p h n", p=P),
+                    out=out[e * C:(e + 1) * C, :].rearrange("(p h) n -> p h n", p=P),
                     in_=y[:, first:first + HALVES, :],
                 )
             elif e % 2 == 1:
                 nc.sync.dma_start(
-                    out=out[(e - 1) * C:(e + 1) * C, :].rearrange("(h p) n -> p h n", p=P),
-                    in_=y[:],
+                    out=out[(e - 1) * C:(e + 1) * C, :].rearrange("(f p h) n -> p f (h n)", p=P, h=HALVES),
+                    in_=y[:].rearrange("p (f h) n -> p f (h n)", h=HALVES),
                 )

@@ -22,9 +22,12 @@ PASSES = K // K_PASS
 HALVES = C // P
 RUN = 4
 CUT = 512
-PARK = 8
-SCALAR_EXPERTS = 4
-RESULT_SLOT = (7, 8, 0, 1)
+PARK = 4
+ALIGN = 256
+SLOT = PACK * N * 4
+SCALAR_PASSES = 6
+RING = 4
+LATE = SCALAR_PASSES + RING
 
 
 def tile_moe_s_lin_relu2_kernel(tc, x_words, x_scales, w, offs, out):
@@ -33,33 +36,38 @@ def tile_moe_s_lin_relu2_kernel(tc, x_words, x_scales, w, offs, out):
         keep = ctx.enter_context(tc.tile_pool(name="keep", bufs=1))
         big = ctx.enter_context(tc.tile_pool(name="big", bufs=1))
         ring = ctx.enter_context(tc.tile_pool(name="ring", bufs=E * PASSES))
-        rounded = ctx.enter_context(tc.tile_pool(name="rounded", bufs=8))
         psum = ctx.enter_context(tc.psum_pool(name="psum", bufs=8))
 
-        offsets = keep.tile([P, E * C // 16], U16, name="offsets", align_bytes=256)
-        words = keep.tile([P, T], I32, name="words", align_bytes=256)
-        scales = keep.tile([P, T // 4], I32, name="scales", align_bytes=256)
-        both = keep.tile([P, E * C], U8, name="both", align_bytes=256)
-        ordered = keep.tile([P, E * C], U8, name="ordered", align_bytes=256)
-        second = keep.tile([P, E * C // 4], I32, name="second", align_bytes=256)
+        offsets = keep.tile([P, E * C // 16], U16, name="offsets", align_bytes=ALIGN)
+        words = keep.tile([P, T], I32, name="words", align_bytes=ALIGN)
+        landed = keep.tile([P, T // 4], I32, name="landed", align_bytes=ALIGN)
+        scales = keep.tile([P, T // 4], I32, name="scales", align_bytes=ALIGN)
+        both = keep.tile([P, E * C], U8, name="both", align_bytes=ALIGN)
+        ordered = keep.tile([P, E * C], U8, name="ordered", align_bytes=ALIGN)
+        second = keep.tile([P, E * C // 4], I32, name="second", align_bytes=ALIGN)
+
+        nc.sync.dma_start(offsets[:], offs)
+        for q in range(4):
+            nc.sync.dma_start(out=landed[32 * q:32 * q + 4, :], in_=x_scales[0, 4 * q:4 * q + 4, :].bitcast(I32))
+        nc.sync.dma_start(out=landed[PARK:PARK + 16, :], in_=x_scales[1].bitcast(I32))
+        nc.sync.dma_start(out=words[:], in_=x_words[0].rearrange("p t d -> p (t d)").bitcast(I32))
+
+        def load(i, dst):
+            e, s = divmod(i, PASSES)
+            nc.sync.dma_start(out=dst, in_=w[e, s * K_PASS:(s + 1) * K_PASS, :].rearrange("(p j) n -> p j n", j=PACK))
+
+        raw = {}
+        for i in range(SCALAR_PASSES):
+            place = i if i <= RING else RING + E * PASSES - LATE
+            raw[i] = big.tile([P, PACK, N], F32, name="raw%d" % i, align_bytes=ALIGN, offset=place * SLOT)[:]
+            load(i, raw[i])
+        last_place = (RING + E * PASSES - LATE) * SLOT
 
         nc.vector.memset(scales[:], 0)
         nc.vector.memset(second[:], 0)
         for q in range(4):
-            nc.scalar.dma_start(out=scales[32 * q:32 * q + 4, :], in_=x_scales[0, 4 * q:4 * q + 4, :].bitcast(I32))
-        nc.scalar.dma_start(out=scales[PARK:PARK + 16, :], in_=x_scales[1].bitcast(I32))
-        nc.sync.dma_start(offsets[:], offs)
-        nc.sync.dma_start(out=words[:], in_=x_words[0].rearrange("p t d -> p (t d)").bitcast(I32))
-
-        raw = {}
-        for e in range(E):
-            for s in range(PASSES):
-                raw[e, s] = big.tile([P, PACK, N], F32, name="big%d" % (PASSES * e + s), align_bytes=256)
-                nc.sync.dma_start(
-                    out=raw[e, s][:],
-                    in_=w[e, s * K_PASS:(s + 1) * K_PASS, :].rearrange("(p j) n -> p j n", j=PACK),
-                )
-
+            rows = slice(32 * q, 32 * q + (PARK + 16 if q == 0 else 4))
+            nc.vector.tensor_copy(out=scales[rows, :], in_=landed[rows, :])
         for c in range(E * C // CUT):
             slots = offsets[:, c * CUT // 16:(c + 1) * CUT // 16]
             nc.vector.tensor_copy(out=both[:, c * CUT:(c + 1) * CUT], in_=scales[:].bitcast(U8).indirect(slots))
@@ -68,11 +76,19 @@ def tile_moe_s_lin_relu2_kernel(tc, x_words, x_scales, w, offs, out):
             in_=both[:].rearrange("p (e m h) -> p e h m", e=E, h=HALVES),
         )
         for q in range(4):
-            nc.gpsimd.dma_start(out=second[32 * q:32 * q + 4, :], in_=ordered[PARK + 4 * q:PARK + 4 * q + 4, :].bitcast(I32))
+            nc.sync.dma_start(out=second[32 * q:32 * q + 4, :], in_=ordered[PARK + 4 * q:PARK + 4 * q + 4, :].bitcast(I32))
         x_scale = [ordered[:], second[:].bitcast(U8)]
 
-        paired = keep.tile([P, E * C], U32, name="paired", align_bytes=256)
-        x_code = keep.tile([P, PASSES, 2 * E * C], U8, name="x_code", align_bytes=256)
+        for i in range(SCALAR_PASSES, LATE):
+            raw[i] = big.tile([P, PACK, N], F32, name="raw%d" % i, align_bytes=ALIGN, offset=(i - SCALAR_PASSES) * SLOT)[:]
+            load(i, raw[i])
+        late = big.tile([P, E * PASSES - LATE, PACK, N], F32, name="late", align_bytes=ALIGN, offset=RING * SLOT)
+        for i in range(LATE, E * PASSES):
+            raw[i] = late[:, i - LATE]
+            load(i, raw[i])
+
+        paired = keep.tile([P, E * C], U32, name="paired", align_bytes=ALIGN)
+        x_code = keep.tile([P, PASSES, 2 * E * C], U8, name="x_code", align_bytes=ALIGN)
         for c in range(E * C // CUT):
             slots = offsets[:, c * CUT // 16:(c + 1) * CUT // 16]
             nc.vector.tensor_copy(out=paired[:, c * CUT:(c + 1) * CUT], in_=words[:].bitcast(U32).indirect(slots))
@@ -82,28 +98,37 @@ def tile_moe_s_lin_relu2_kernel(tc, x_words, x_scales, w, offs, out):
                 in_=paired[:, c * CUT:(c + 1) * CUT].bitcast(U16).rearrange("p (e m h s) -> p s e h m", s=PASSES, h=HALVES, m=P),
             )
 
-        for e in range(E):
+        def views(g, i, cols):
+            dst = g.rearrange("p (c i) t -> p c t i", i=RUN)
+            src = raw[i][:, :, cols].rearrange("p t (c i) -> p c t i", i=RUN)
+            return dst, src
 
-            grouped = []
-            for s in range(PASSES):
-                g = rounded.tile([P, N, PACK], BF16, name="grouped", align_bytes=256)
-                dst = g[:].rearrange("p (c i) t -> p c t i", i=RUN)
-                src = raw[e, s][:].rearrange("p t (c i) -> p c t i", i=RUN)
-                if e < SCALAR_EXPERTS:
-                    nc.scalar.activation(out=dst, in_=src, func=ACT.Copy)
-                else:
-                    nc.vector.tensor_copy(out=dst, in_=src)
-                grouped.append(g)
+        for e in range(E):
             w_code = []
             w_scale = []
             for s in range(PASSES):
-                code = ring.tile([P, N], U32, name="w_code", align_bytes=256)
-                scale = ring.tile([P, N], U8, name="w_scale", align_bytes=256)
-                nc.vector.quantize_mx(
-                    out=code[:].bitcast(FP8X4),
-                    scales=scale[:],
-                    in_=grouped[s][:].rearrange("p n t -> p (n t)"),
-                )
+                i = PASSES * e + s
+                code = ring.tile([P, N], U32, name="w_code", align_bytes=ALIGN)
+                scale = ring.tile([P, N], U8, name="w_scale", align_bytes=ALIGN)
+                if i < SCALAR_PASSES:
+                    g = keep.tile([P, N, PACK], BF16, name="grouped%d" % i, align_bytes=ALIGN)
+                    dst, src = views(g[:], i, slice(0, N))
+                    nc.scalar.activation(out=dst, in_=src, func=ACT.Copy)
+                    parts = [(slice(0, N), g)]
+                else:
+                    parts = []
+                    for u in range(2):
+                        cols = slice(u * N // 2, (u + 1) * N // 2)
+                        g = big.tile([P, N // 2, PACK], BF16, name="grouped%d_%d" % (i, u), align_bytes=ALIGN, offset=last_place + u * SLOT // 4)
+                        dst, src = views(g[:], i, cols)
+                        nc.vector.tensor_copy(out=dst, in_=src)
+                        parts.append((cols, g))
+                for cols, g in parts:
+                    nc.vector.quantize_mx(
+                        out=code[:, cols].bitcast(FP8X4),
+                        scales=scale[:, cols],
+                        in_=g[:].rearrange("p n t -> p (n t)"),
+                    )
                 w_code.append(code)
                 w_scale.append(scale)
 
@@ -120,14 +145,15 @@ def tile_moe_s_lin_relu2_kernel(tc, x_words, x_scales, w, offs, out):
                         stop=(s == PASSES - 1),
                     )
             if e % 2 == 0:
-                y = big.tile([P, 2 * HALVES, N], F32, name="big%d" % RESULT_SLOT[e // 2], align_bytes=256)
+                place = last_place + SLOT // 2 if e == 0 else (e // 2 - 1) * SLOT
+                y = big.tile([P, 2 * HALVES, N], F32, name="y%d" % e, align_bytes=ALIGN, offset=place)
             first = (e % 2) * HALVES
             if e == E - 1:
                 positive = keep.tile([P, N], F32, name="positive")
-                nc.scalar.activation(out=y[:, first, :], in_=acc[0][:], func=ACT.Relu)
-                nc.vector.tensor_scalar_max(positive[:], acc[1][:], 0.0)
-                nc.scalar.activation(out=y[:, first, :], in_=y[:, first, :], func=ACT.Square)
-                nc.vector.tensor_tensor(y[:, first + 1, :], positive[:], positive[:], mybir.AluOpType.mult)
+                nc.vector.tensor_scalar_max(positive[:], acc[0][:], 0.0)
+                nc.scalar.activation(out=y[:, first + 1, :], in_=acc[1][:], func=ACT.Relu)
+                nc.vector.tensor_tensor(y[:, first, :], positive[:], positive[:], mybir.AluOpType.mult)
+                nc.scalar.activation(out=y[:, first + 1, :], in_=y[:, first + 1, :], func=ACT.Square)
             else:
                 for h in range(HALVES):
                     nc.scalar.activation(out=y[:, first + h, :], in_=acc[h][:], func=ACT.Relu)

@@ -47,8 +47,8 @@ def tile_moe_s_lin_relu2_kernel(tc, x_words, x_scales, w, offs, out):
         second = keep.tile([P, E * C // 4], I32, name="second", align_bytes=ALIGN)
 
         nc.sync.dma_start(offsets[:], offs)
-        for q in range(4):
-            nc.sync.dma_start(out=landed[32 * q:32 * q + 4, :], in_=x_scales[0, 4 * q:4 * q + 4, :].bitcast(I32))
+        for r in range(4):
+            nc.sync.dma_start(out=landed[r:P:32, :], in_=x_scales[0, r:16:4, :].bitcast(I32))
         nc.sync.dma_start(out=landed[PARK:PARK + 16, :], in_=x_scales[1].bitcast(I32))
         nc.sync.dma_start(out=words[:], in_=x_words[0].rearrange("p t d -> p (t d)").bitcast(I32))
 
@@ -75,8 +75,8 @@ def tile_moe_s_lin_relu2_kernel(tc, x_words, x_scales, w, offs, out):
             out=ordered[:].rearrange("p (e h m) -> p e h m", e=E, h=HALVES),
             in_=both[:].rearrange("p (e m h) -> p e h m", e=E, h=HALVES),
         )
-        for q in range(4):
-            nc.sync.dma_start(out=second[32 * q:32 * q + 4, :], in_=ordered[PARK + 4 * q:PARK + 4 * q + 4, :].bitcast(I32))
+        for r in range(4):
+            nc.sync.dma_start(out=second[r:P:32, :], in_=ordered[PARK + r:PARK + 16:4, :].bitcast(I32))
         x_scale = [ordered[:], second[:].bitcast(U8)]
 
         for i in range(SCALAR_PASSES, LATE):

@@ -28,6 +28,8 @@ SLOT = PACK * N * 4
 SCALAR_PASSES = 6
 RING = 4
 LATE = SCALAR_PASSES + RING
+SHARED = (6, 7)
+RESULT_SLOT = (1, 0, 2, 3)
 
 
 def tile_moe_s_lin_relu2_kernel(tc, x_words, x_scales, w, offs, out):
@@ -43,14 +45,13 @@ def tile_moe_s_lin_relu2_kernel(tc, x_words, x_scales, w, offs, out):
         landed = keep.tile([P, T // 4], I32, name="landed", align_bytes=ALIGN)
         scales = keep.tile([P, T // 4], I32, name="scales", align_bytes=ALIGN)
         both = keep.tile([P, E * C], U8, name="both", align_bytes=ALIGN)
-        ordered = keep.tile([P, E * C], U8, name="ordered", align_bytes=ALIGN)
         second = keep.tile([P, E * C // 4], I32, name="second", align_bytes=ALIGN)
 
-        nc.sync.dma_start(offsets[:], offs)
+        nc.sync.dma_start(out=words[:], in_=x_words[0].rearrange("p t d -> p (t d)").bitcast(I32))
         for r in range(4):
             nc.sync.dma_start(out=landed[r:P:32, :], in_=x_scales[0, r:16:4, :].bitcast(I32))
         nc.sync.dma_start(out=landed[PARK:PARK + 16, :], in_=x_scales[1].bitcast(I32))
-        nc.sync.dma_start(out=words[:], in_=x_words[0].rearrange("p t d -> p (t d)").bitcast(I32))
+        nc.sync.dma_start(offsets[:], offs)
 
         def load(i, dst):
             e, s = divmod(i, PASSES)
@@ -71,13 +72,9 @@ def tile_moe_s_lin_relu2_kernel(tc, x_words, x_scales, w, offs, out):
         for c in range(E * C // CUT):
             slots = offsets[:, c * CUT // 16:(c + 1) * CUT // 16]
             nc.vector.tensor_copy(out=both[:, c * CUT:(c + 1) * CUT], in_=scales[:].bitcast(U8).indirect(slots))
-        nc.vector.tensor_copy(
-            out=ordered[:].rearrange("p (e h m) -> p e h m", e=E, h=HALVES),
-            in_=both[:].rearrange("p (e m h) -> p e h m", e=E, h=HALVES),
-        )
         for r in range(4):
-            nc.sync.dma_start(out=second[r:P:32, :], in_=ordered[PARK + r:PARK + 16:4, :].bitcast(I32))
-        x_scale = [ordered[:], second[:].bitcast(U8)]
+            nc.sync.dma_start(out=second[r:P:32, :], in_=both[PARK + r:PARK + 16:4, :].bitcast(I32))
+        x_scale = [both[:], second[:].bitcast(U8)]
 
         for i in range(SCALAR_PASSES, LATE):
             raw[i] = big.tile([P, PACK, N], F32, name="raw%d" % i, align_bytes=ALIGN, offset=(i - SCALAR_PASSES) * SLOT)[:]
@@ -94,8 +91,8 @@ def tile_moe_s_lin_relu2_kernel(tc, x_words, x_scales, w, offs, out):
             nc.vector.tensor_copy(out=paired[:, c * CUT:(c + 1) * CUT], in_=words[:].bitcast(U32).indirect(slots))
         for c in range(E * C // CUT):
             nc.vector.tensor_copy(
-                out=x_code[:, :, 2 * c * CUT:2 * (c + 1) * CUT].bitcast(U16).rearrange("p s (e h m) -> p s e h m", h=HALVES, m=P),
-                in_=paired[:, c * CUT:(c + 1) * CUT].bitcast(U16).rearrange("p (e m h s) -> p s e h m", s=PASSES, h=HALVES, m=P),
+                out=x_code[:, :, 2 * c * CUT:2 * (c + 1) * CUT].bitcast(U16),
+                in_=paired[:, c * CUT:(c + 1) * CUT].bitcast(U16).rearrange("p (u s) -> p s u", s=PASSES),
             )
 
         def views(g, i, cols):
@@ -103,69 +100,85 @@ def tile_moe_s_lin_relu2_kernel(tc, x_words, x_scales, w, offs, out):
             src = raw[i][:, :, cols].rearrange("p t (c i) -> p c t i", i=RUN)
             return dst, src
 
-        for e in range(E):
-            w_code = []
-            w_scale = []
-            for s in range(PASSES):
-                i = PASSES * e + s
-                code = ring.tile([P, N], U32, name="w_code", align_bytes=ALIGN)
-                scale = ring.tile([P, N], U8, name="w_scale", align_bytes=ALIGN)
-                if i < SCALAR_PASSES:
-                    g = keep.tile([P, N, PACK], BF16, name="grouped%d" % i, align_bytes=ALIGN)
-                    dst, src = views(g[:], i, slice(0, N))
-                    nc.scalar.activation(out=dst, in_=src, func=ACT.Copy)
-                    parts = [(slice(0, N), g)]
-                else:
-                    parts = []
-                    for u in range(2):
-                        cols = slice(u * N // 2, (u + 1) * N // 2)
-                        g = big.tile([P, N // 2, PACK], BF16, name="grouped%d_%d" % (i, u), align_bytes=ALIGN, offset=last_place + u * SLOT // 4)
-                        dst, src = views(g[:], i, cols)
-                        nc.vector.tensor_copy(out=dst, in_=src)
-                        parts.append((cols, g))
-                for cols, g in parts:
-                    nc.vector.quantize_mx(
-                        out=code[:, cols].bitcast(FP8X4),
-                        scales=scale[:, cols],
-                        in_=g[:].rearrange("p n t -> p (n t)"),
-                    )
-                w_code.append(code)
-                w_scale.append(scale)
+        def quantise(code, scale, cols, g):
+            nc.vector.quantize_mx(
+                out=code[:, cols].bitcast(FP8X4),
+                scales=scale[:, cols],
+                in_=g[:].rearrange("p n t -> p (n t)"),
+            )
 
-            acc = [psum.tile([P, N], F32, name="acc") for h in range(HALVES)]
-            for s in range(PASSES):
-                for h in range(HALVES):
-                    nc.tensor.matmul_mx(
-                        out=acc[h][:],
-                        lhsT=x_code[:, s, 2 * (C * e + P * h):2 * (C * e + P * (h + 1))].bitcast(FP4X4),
-                        lhsT_scale=x_scale[s][:, C * e + P * h:C * e + P * (h + 1)],
-                        rhs=w_code[s][:].bitcast(FP8X4),
-                        rhs_scale=w_scale[s][:],
-                        start=(s == 0),
-                        stop=(s == PASSES - 1),
-                    )
+        def quantised(i):
+            code = ring.tile([P, N], U32, name="w_code", align_bytes=ALIGN)
+            scale = ring.tile([P, N], U8, name="w_scale", align_bytes=ALIGN)
+            if i < SCALAR_PASSES:
+                g = keep.tile([P, N, PACK], BF16, name="grouped%d" % i, align_bytes=ALIGN)
+                dst, src = views(g[:], i, slice(0, N))
+                nc.scalar.activation(out=dst, in_=src, func=ACT.Copy)
+                parts = [(slice(0, N), g)]
+            else:
+                parts = []
+                for u in range(2):
+                    g = big.tile([P, N // 2, PACK], BF16, name="grouped%d_%d" % (i, u), align_bytes=ALIGN, offset=last_place + u * SLOT // 4)
+                    parts.append((slice(u * N // 2, (u + 1) * N // 2), g))
+                for cols, g in parts:
+                    dst, src = views(g[:], i, cols)
+                    if i in SHARED and cols.start > 0:
+                        nc.scalar.activation(out=dst, in_=src, func=ACT.Copy)
+                    else:
+                        nc.vector.tensor_copy(out=dst, in_=src)
+            for cols, g in parts:
+                quantise(code, scale, cols, g)
+            return code, scale
+
+        def multiply(acc, e, s, code, scale):
+            for h in range(HALVES):
+                nc.tensor.matmul_mx(
+                    out=acc[h][:],
+                    lhsT=x_code[:, s, 2 * (C * e + P * h):2 * (C * e + P * (h + 1))].bitcast(FP4X4),
+                    lhsT_scale=x_scale[s][:, C * e + P * h:C * e + P * (h + 1)],
+                    rhs=code[:].bitcast(FP8X4),
+                    rhs_scale=scale[:],
+                    start=(s == 0),
+                    stop=(s == PASSES - 1),
+                )
+
+        pairs = {}
+
+        def finish(e, acc):
             if e % 2 == 0:
-                place = last_place + SLOT // 2 if e == 0 else (e // 2 - 1) * SLOT
-                y = big.tile([P, 2 * HALVES, N], F32, name="y%d" % e, align_bytes=ALIGN, offset=place)
+                place = RESULT_SLOT[e // 2] * SLOT
+                pairs[e // 2] = big.tile([P, 2 * HALVES, N], F32, name="y%d" % e, align_bytes=ALIGN, offset=place)
+            y = pairs[e // 2]
             first = (e % 2) * HALVES
+            rows = out[e * C:(e + 1) * C, :].rearrange("(h p) n -> p h n", p=P)
             if e == E - 1:
                 positive = keep.tile([P, N], F32, name="positive")
                 nc.vector.tensor_scalar_max(positive[:], acc[0][:], 0.0)
                 nc.scalar.activation(out=y[:, first + 1, :], in_=acc[1][:], func=ACT.Relu)
                 nc.vector.tensor_tensor(y[:, first, :], positive[:], positive[:], mybir.AluOpType.mult)
                 nc.scalar.activation(out=y[:, first + 1, :], in_=y[:, first + 1, :], func=ACT.Square)
-            else:
                 for h in range(HALVES):
-                    nc.scalar.activation(out=y[:, first + h, :], in_=acc[h][:], func=ACT.Relu)
-                for h in range(HALVES):
-                    nc.scalar.activation(out=y[:, first + h, :], in_=y[:, first + h, :], func=ACT.Square)
-            if e >= E - 2:
-                nc.sync.dma_start(
-                    out=out[e * C:(e + 1) * C, :].rearrange("(p h) n -> p h n", p=P),
-                    in_=y[:, first:first + HALVES, :],
-                )
+                    nc.sync.dma_start(out=rows[:, h, :], in_=y[:, first + h, :])
+                return
+            for h in range(HALVES):
+                nc.scalar.activation(out=y[:, first + h, :], in_=acc[h][:], func=ACT.Relu)
+            for h in range(HALVES):
+                nc.scalar.activation(out=y[:, first + h, :], in_=y[:, first + h, :], func=ACT.Square)
+            if e == E - 2:
+                nc.sync.dma_start(out=rows, in_=y[:, first:first + HALVES, :])
             elif e % 2 == 1:
                 nc.sync.dma_start(
-                    out=out[(e - 1) * C:(e + 1) * C, :].rearrange("(f p h) n -> p f (h n)", p=P, h=HALVES),
-                    in_=y[:].rearrange("p (f h) n -> p f (h n)", h=HALVES),
+                    out=out[(e - 1) * C:(e + 1) * C, :].rearrange("(h p) n -> p h n", p=P),
+                    in_=y[:],
                 )
+
+        done = None
+        for e in range(E):
+            acc = [psum.tile([P, N], F32, name="acc") for h in range(HALVES)]
+            for s in range(PASSES):
+                code, scale = quantised(PASSES * e + s)
+                if s == 0 and e > 0:
+                    finish(e - 1, done)
+                multiply(acc, e, s, code, scale)
+            done = acc
+        finish(E - 1, done)

@@ -22,14 +22,11 @@ PASSES = K // K_PASS
 HALVES = C // P
 RUN = 4
 CUT = 512
-PARK = 4
 ALIGN = 256
 SLOT = PACK * N * 4
-SCALAR_PASSES = 6
-RING = 4
+SCALAR_PASSES = 8
+RING = 6
 LATE = SCALAR_PASSES + RING
-SHARED = (6, 7)
-RESULT_SLOT = (1, 0, 2, 3)
 
 
 def tile_moe_s_lin_relu2_kernel(tc, x_words, x_scales, w, offs, out):
@@ -42,16 +39,20 @@ def tile_moe_s_lin_relu2_kernel(tc, x_words, x_scales, w, offs, out):
 
         offsets = keep.tile([P, E * C // 16], U16, name="offsets", align_bytes=ALIGN)
         words = keep.tile([P, T], I32, name="words", align_bytes=ALIGN)
-        landed = keep.tile([P, T // 4], I32, name="landed", align_bytes=ALIGN)
-        scales = keep.tile([P, T // 4], I32, name="scales", align_bytes=ALIGN)
-        both = keep.tile([P, E * C], U8, name="both", align_bytes=ALIGN)
-        second = keep.tile([P, E * C // 4], I32, name="second", align_bytes=ALIGN)
+        landed = keep.tile([P, PASSES * T // 4], I32, name="landed", align_bytes=ALIGN)
+        scales = keep.tile([P, PASSES * T // 4], I32, name="scales", align_bytes=ALIGN)
+        x_scale = [keep.tile([P, E * C], U8, name="x_scale%d" % s, align_bytes=ALIGN) for s in range(PASSES)]
 
         nc.sync.dma_start(out=words[:], in_=x_words[0].rearrange("p t d -> p (t d)").bitcast(I32))
         for r in range(4):
-            nc.sync.dma_start(out=landed[r:P:32, :], in_=x_scales[0, r:16:4, :].bitcast(I32))
-        nc.sync.dma_start(out=landed[PARK:PARK + 16, :], in_=x_scales[1].bitcast(I32))
+            nc.sync.dma_start(
+                out=landed[r:P:32, :].rearrange("q (s t) -> q s t", s=PASSES),
+                in_=x_scales[:, r:16:4, :].bitcast(I32).rearrange("s q t -> q s t"),
+            )
         nc.sync.dma_start(offsets[:], offs)
+        nc.vector.memset(scales[:], 0)
+        for q in range(4):
+            nc.vector.tensor_copy(out=scales[32 * q:32 * q + 4, :], in_=landed[32 * q:32 * q + 4, :])
 
         def load(i, dst):
             e, s = divmod(i, PASSES)
@@ -63,18 +64,6 @@ def tile_moe_s_lin_relu2_kernel(tc, x_words, x_scales, w, offs, out):
             raw[i] = big.tile([P, PACK, N], F32, name="raw%d" % i, align_bytes=ALIGN, offset=place * SLOT)[:]
             load(i, raw[i])
         last_place = (RING + E * PASSES - LATE) * SLOT
-
-        nc.vector.memset(scales[:], 0)
-        nc.vector.memset(second[:], 0)
-        for q in range(4):
-            rows = slice(32 * q, 32 * q + (PARK + 16 if q == 0 else 4))
-            nc.vector.tensor_copy(out=scales[rows, :], in_=landed[rows, :])
-        for c in range(E * C // CUT):
-            slots = offsets[:, c * CUT // 16:(c + 1) * CUT // 16]
-            nc.vector.tensor_copy(out=both[:, c * CUT:(c + 1) * CUT], in_=scales[:].bitcast(U8).indirect(slots))
-        for r in range(4):
-            nc.sync.dma_start(out=second[r:P:32, :], in_=both[PARK + r:PARK + 16:4, :].bitcast(I32))
-        x_scale = [both[:], second[:].bitcast(U8)]
 
         for i in range(SCALAR_PASSES, LATE):
             raw[i] = big.tile([P, PACK, N], F32, name="raw%d" % i, align_bytes=ALIGN, offset=(i - SCALAR_PASSES) * SLOT)[:]
@@ -94,6 +83,11 @@ def tile_moe_s_lin_relu2_kernel(tc, x_words, x_scales, w, offs, out):
                 out=x_code[:, :, 2 * c * CUT:2 * (c + 1) * CUT].bitcast(U16),
                 in_=paired[:, c * CUT:(c + 1) * CUT].bitcast(U16).rearrange("p (u s) -> p s u", s=PASSES),
             )
+        for c in range(E * C // CUT):
+            slots = offsets[:, c * CUT // 16:(c + 1) * CUT // 16]
+            for s in range(PASSES):
+                window = scales[:].bitcast(U8)[:, s * T:(s + 1) * T]
+                nc.vector.tensor_copy(out=x_scale[s][:, c * CUT:(c + 1) * CUT], in_=window.indirect(slots))
 
         def views(g, i, cols):
             dst = g.rearrange("p (c i) t -> p c t i", i=RUN)
@@ -122,10 +116,7 @@ def tile_moe_s_lin_relu2_kernel(tc, x_words, x_scales, w, offs, out):
                     parts.append((slice(u * N // 2, (u + 1) * N // 2), g))
                 for cols, g in parts:
                     dst, src = views(g[:], i, cols)
-                    if i in SHARED and cols.start > 0:
-                        nc.scalar.activation(out=dst, in_=src, func=ACT.Copy)
-                    else:
-                        nc.vector.tensor_copy(out=dst, in_=src)
+                    nc.vector.tensor_copy(out=dst, in_=src)
             for cols, g in parts:
                 quantise(code, scale, cols, g)
             return code, scale
@@ -146,7 +137,7 @@ def tile_moe_s_lin_relu2_kernel(tc, x_words, x_scales, w, offs, out):
 
         def finish(e, acc):
             if e % 2 == 0:
-                place = RESULT_SLOT[e // 2] * SLOT
+                place = last_place + SLOT // 2 if e == 0 else (e // 2 - 1) * SLOT
                 pairs[e // 2] = big.tile([P, 2 * HALVES, N], F32, name="y%d" % e, align_bytes=ALIGN, offset=place)
             y = pairs[e // 2]
             first = (e % 2) * HALVES

@@ -24,9 +24,9 @@ RUN = 4
 CUT = 512
 ALIGN = 256
 SLOT = PACK * N * 4
-SCALAR_PASSES = 8
-RING = 6
-LATE = SCALAR_PASSES + RING
+SCALAR_PASSES = 7
+LOADS = [1, 1, 2, 2, 2, 2, 2, 1, 1, 1, 1]
+STORES = [4, 2, 1, 1]
 
 
 def tile_moe_s_lin_relu2_kernel(tc, x_words, x_scales, w, offs, out):
@@ -39,39 +39,27 @@ def tile_moe_s_lin_relu2_kernel(tc, x_words, x_scales, w, offs, out):
 
         offsets = keep.tile([P, E * C // 16], U16, name="offsets", align_bytes=ALIGN)
         words = keep.tile([P, T], I32, name="words", align_bytes=ALIGN)
-        landed = keep.tile([P, PASSES * T // 4], I32, name="landed", align_bytes=ALIGN)
         scales = keep.tile([P, PASSES * T // 4], I32, name="scales", align_bytes=ALIGN)
         x_scale = [keep.tile([P, E * C], U8, name="x_scale%d" % s, align_bytes=ALIGN) for s in range(PASSES)]
 
+        nc.vector.memset(scales[:], 0)
+        nc.sync.dma_start(offsets[:], offs)
         nc.sync.dma_start(out=words[:], in_=x_words[0].rearrange("p t d -> p (t d)").bitcast(I32))
         for r in range(4):
             nc.sync.dma_start(
-                out=landed[r:P:32, :].rearrange("q (s t) -> q s t", s=PASSES),
+                out=scales[r:P:32, :].rearrange("q (s t) -> q s t", s=PASSES),
                 in_=x_scales[:, r:16:4, :].bitcast(I32).rearrange("s q t -> q s t"),
             )
-        nc.sync.dma_start(offsets[:], offs)
-        nc.vector.memset(scales[:], 0)
-        for q in range(4):
-            nc.vector.tensor_copy(out=scales[32 * q:32 * q + 4, :], in_=landed[32 * q:32 * q + 4, :])
 
-        def load(i, dst):
-            e, s = divmod(i, PASSES)
-            nc.sync.dma_start(out=dst, in_=w[e, s * K_PASS:(s + 1) * K_PASS, :].rearrange("(p j) n -> p j n", j=PACK))
-
+        rows_k = w.rearrange("e (s p j) n -> p (e s) j n", p=P, j=PACK)
         raw = {}
-        for i in range(SCALAR_PASSES):
-            place = i if i <= RING else RING + E * PASSES - LATE
-            raw[i] = big.tile([P, PACK, N], F32, name="raw%d" % i, align_bytes=ALIGN, offset=place * SLOT)[:]
-            load(i, raw[i])
-        last_place = (RING + E * PASSES - LATE) * SLOT
-
-        for i in range(SCALAR_PASSES, LATE):
-            raw[i] = big.tile([P, PACK, N], F32, name="raw%d" % i, align_bytes=ALIGN, offset=(i - SCALAR_PASSES) * SLOT)[:]
-            load(i, raw[i])
-        late = big.tile([P, E * PASSES - LATE, PACK, N], F32, name="late", align_bytes=ALIGN, offset=RING * SLOT)
-        for i in range(LATE, E * PASSES):
-            raw[i] = late[:, i - LATE]
-            load(i, raw[i])
+        first_pass = 0
+        for count in LOADS:
+            part = big.tile([P, count, PACK, N], F32, name="raw%d" % first_pass, align_bytes=ALIGN, offset=first_pass * SLOT)
+            nc.sync.dma_start(out=part[:], in_=rows_k[:, first_pass:first_pass + count])
+            for i in range(count):
+                raw[first_pass + i] = part[:, i]
+            first_pass = first_pass + count
 
         paired = keep.tile([P, E * C], U32, name="paired", align_bytes=ALIGN)
         x_code = keep.tile([P, PASSES, 2 * E * C], U8, name="x_code", align_bytes=ALIGN)
@@ -112,7 +100,7 @@ def tile_moe_s_lin_relu2_kernel(tc, x_words, x_scales, w, offs, out):
             else:
                 parts = []
                 for u in range(2):
-                    g = big.tile([P, N // 2, PACK], BF16, name="grouped%d_%d" % (i, u), align_bytes=ALIGN, offset=last_place + u * SLOT // 4)
+                    g = big.tile([P, N // 2, PACK], BF16, name="grouped%d_%d" % (i, u), align_bytes=ALIGN, offset=E * PASSES * SLOT + u * SLOT // 4)
                     parts.append((slice(u * N // 2, (u + 1) * N // 2), g))
                 for cols, g in parts:
                     dst, src = views(g[:], i, cols)
@@ -133,16 +121,23 @@ def tile_moe_s_lin_relu2_kernel(tc, x_words, x_scales, w, offs, out):
                     stop=(s == PASSES - 1),
                 )
 
-        pairs = {}
+        group = {}
+        first_expert = 0
+        for g, count in enumerate(STORES):
+            for e in range(first_expert, first_expert + count):
+                group[e] = (g, first_expert, count)
+            first_expert = first_expert + count
+        places = [6 * SLOT, 0, SLOT, SLOT + SLOT // 2]
+        results = {}
 
         def finish(e, acc):
-            if e % 2 == 0:
-                place = last_place + SLOT // 2 if e == 0 else (e // 2 - 1) * SLOT
-                pairs[e // 2] = big.tile([P, 2 * HALVES, N], F32, name="y%d" % e, align_bytes=ALIGN, offset=place)
-            y = pairs[e // 2]
-            first = (e % 2) * HALVES
-            rows = out[e * C:(e + 1) * C, :].rearrange("(h p) n -> p h n", p=P)
+            g, start, count = group[e]
+            if e == start:
+                results[g] = big.tile([P, count * HALVES, N], F32, name="y%d" % e, align_bytes=ALIGN, offset=places[g])
+            y = results[g]
+            first = (e - start) * HALVES
             if e == E - 1:
+                rows = out[e * C:(e + 1) * C, :].rearrange("(h p) n -> p h n", p=P)
                 positive = keep.tile([P, N], F32, name="positive")
                 nc.vector.tensor_scalar_max(positive[:], acc[0][:], 0.0)
                 nc.scalar.activation(out=y[:, first + 1, :], in_=acc[1][:], func=ACT.Relu)
@@ -153,13 +148,11 @@ def tile_moe_s_lin_relu2_kernel(tc, x_words, x_scales, w, offs, out):
                 return
             for h in range(HALVES):
                 nc.scalar.activation(out=y[:, first + h, :], in_=acc[h][:], func=ACT.Relu)
-            for h in range(HALVES):
-                nc.scalar.activation(out=y[:, first + h, :], in_=y[:, first + h, :], func=ACT.Square)
-            if e == E - 2:
-                nc.sync.dma_start(out=rows, in_=y[:, first:first + HALVES, :])
-            elif e % 2 == 1:
+            both = y[:, first:first + HALVES, :]
+            nc.scalar.activation(out=both, in_=both, func=ACT.Square)
+            if e == start + count - 1:
                 nc.sync.dma_start(
-                    out=out[(e - 1) * C:(e + 1) * C, :].rearrange("(h p) n -> p h n", p=P),
+                    out=out[start * C:(e + 1) * C, :].rearrange("(h p) n -> p h n", p=P),
                     in_=y[:],
                 )
 

@@ -26,7 +26,7 @@ ALIGN = 256
 SLOT = PACK * N * 4
 SCALAR_PASSES = 7
 LOADS = [1, 1, 2, 2, 2, 2, 2, 1, 1, 1, 1]
-STORES = [4, 2, 1, 1]
+STORES = [4, 2, 1]
 
 
 def tile_moe_s_lin_relu2_kernel(tc, x_words, x_scales, w, offs, out):
@@ -43,13 +43,8 @@ def tile_moe_s_lin_relu2_kernel(tc, x_words, x_scales, w, offs, out):
         x_scale = [keep.tile([P, E * C], U8, name="x_scale%d" % s, align_bytes=ALIGN) for s in range(PASSES)]
 
         nc.vector.memset(scales[:], 0)
-        nc.sync.dma_start(offsets[:], offs)
         nc.sync.dma_start(out=words[:], in_=x_words[0].rearrange("p t d -> p (t d)").bitcast(I32))
-        for r in range(4):
-            nc.sync.dma_start(
-                out=scales[r:P:32, :].rearrange("q (s t) -> q s t", s=PASSES),
-                in_=x_scales[:, r:16:4, :].bitcast(I32).rearrange("s q t -> q s t"),
-            )
+        nc.sync.dma_start(offsets[:], offs)
 
         rows_k = w.rearrange("e (s p j) n -> p (e s) j n", p=P, j=PACK)
         raw = {}
@@ -57,6 +52,12 @@ def tile_moe_s_lin_relu2_kernel(tc, x_words, x_scales, w, offs, out):
         for count in LOADS:
             part = big.tile([P, count, PACK, N], F32, name="raw%d" % first_pass, align_bytes=ALIGN, offset=first_pass * SLOT)
             nc.sync.dma_start(out=part[:], in_=rows_k[:, first_pass:first_pass + count])
+            if first_pass == 0:
+                for r in range(4):
+                    nc.sync.dma_start(
+                        out=scales[r:P:32, :].rearrange("q (s t) -> q s t", s=PASSES),
+                        in_=x_scales[:, r:16:4, :].bitcast(I32).rearrange("s q t -> q s t"),
+                    )
             for i in range(count):
                 raw[first_pass + i] = part[:, i]
             first_pass = first_pass + count
@@ -109,17 +110,16 @@ def tile_moe_s_lin_relu2_kernel(tc, x_words, x_scales, w, offs, out):
                 quantise(code, scale, cols, g)
             return code, scale
 
-        def multiply(acc, e, s, code, scale):
-            for h in range(HALVES):
-                nc.tensor.matmul_mx(
-                    out=acc[h][:],
-                    lhsT=x_code[:, s, 2 * (C * e + P * h):2 * (C * e + P * (h + 1))].bitcast(FP4X4),
-                    lhsT_scale=x_scale[s][:, C * e + P * h:C * e + P * (h + 1)],
-                    rhs=code[:].bitcast(FP8X4),
-                    rhs_scale=scale[:],
-                    start=(s == 0),
-                    stop=(s == PASSES - 1),
-                )
+        def multiply(acc, e, s, h, code, scale, cols):
+            nc.tensor.matmul_mx(
+                out=acc[:],
+                lhsT=x_code[:, s, 2 * (C * e + P * h):2 * (C * e + P * (h + 1))].bitcast(FP4X4),
+                lhsT_scale=x_scale[s][:, C * e + P * h:C * e + P * (h + 1)],
+                rhs=code[:, cols].bitcast(FP8X4),
+                rhs_scale=scale[:, cols],
+                start=(s == 0),
+                stop=(s == PASSES - 1),
+            )
 
         group = {}
         first_expert = 0
@@ -136,16 +136,6 @@ def tile_moe_s_lin_relu2_kernel(tc, x_words, x_scales, w, offs, out):
                 results[g] = big.tile([P, count * HALVES, N], F32, name="y%d" % e, align_bytes=ALIGN, offset=places[g])
             y = results[g]
             first = (e - start) * HALVES
-            if e == E - 1:
-                rows = out[e * C:(e + 1) * C, :].rearrange("(h p) n -> p h n", p=P)
-                positive = keep.tile([P, N], F32, name="positive")
-                nc.vector.tensor_scalar_max(positive[:], acc[0][:], 0.0)
-                nc.scalar.activation(out=y[:, first + 1, :], in_=acc[1][:], func=ACT.Relu)
-                nc.vector.tensor_tensor(y[:, first, :], positive[:], positive[:], mybir.AluOpType.mult)
-                nc.scalar.activation(out=y[:, first + 1, :], in_=y[:, first + 1, :], func=ACT.Square)
-                for h in range(HALVES):
-                    nc.sync.dma_start(out=rows[:, h, :], in_=y[:, first + h, :])
-                return
             for h in range(HALVES):
                 nc.scalar.activation(out=y[:, first + h, :], in_=acc[h][:], func=ACT.Relu)
             both = y[:, first:first + HALVES, :]
@@ -157,12 +147,33 @@ def tile_moe_s_lin_relu2_kernel(tc, x_words, x_scales, w, offs, out):
                 )
 
         done = None
-        for e in range(E):
+        for e in range(E - 1):
             acc = [psum.tile([P, N], F32, name="acc") for h in range(HALVES)]
             for s in range(PASSES):
                 code, scale = quantised(PASSES * e + s)
                 if s == 0 and e > 0:
                     finish(e - 1, done)
-                multiply(acc, e, s, code, scale)
+                for h in range(HALVES):
+                    multiply(acc[h], e, s, h, code, scale, slice(0, N))
             done = acc
-        finish(E - 1, done)
+
+        e = E - 1
+        order = [(u, h, b) for u in range(2) for h in range(HALVES) for b in range(2)]
+        acc = {key: psum.tile([P, P], F32, name="acc") for key in order}
+        for s in range(PASSES):
+            code, scale = quantised(PASSES * e + s)
+            if s == 0:
+                finish(e - 1, done)
+            for u, h, b in order:
+                multiply(acc[u, h, b], e, s, h, code, scale, slice((2 * u + b) * P, (2 * u + b + 1) * P))
+        y = big.tile([P, HALVES, N], F32, name="y_last", align_bytes=ALIGN, offset=places[-1])
+        positive = keep.tile([P, N], F32, name="positive")
+        for u in range(2):
+            cols = slice(u * N // 2, (u + 1) * N // 2)
+            for b in range(2):
+                block = slice((2 * u + b) * P, (2 * u + b + 1) * P)
+                nc.scalar.activation(out=y[:, 0, block], in_=acc[u, 0, b][:], func=ACT.Relu)
+                nc.vector.tensor_scalar_max(positive[:, block], acc[u, 1, b][:], 0.0)
+            nc.scalar.activation(out=y[:, 0, cols], in_=y[:, 0, cols], func=ACT.Square)
+            nc.vector.tensor_tensor(y[:, 1, cols], positive[:, cols], positive[:, cols], mybir.AluOpType.mult)
+        nc.sync.dma_start(out=out[e * C:(e + 1) * C, :].rearrange("(h p) n -> p h n", p=P), in_=y[:])

@@ -27,6 +27,7 @@ SLOT = PACK * N * 4
 SCALAR_PASSES = 7
 LOADS = [1, 1, 2, 2, 2, 2, 2, 1, 1, 1, 1]
 STORES = [4, 2, 1]
+LOW_ENGINES = [(0, 44), (44, 88), (88, 128)]
 
 
 def tile_moe_s_lin_relu2_kernel(tc, x_words, x_scales, w, offs, out):
@@ -141,10 +142,13 @@ def tile_moe_s_lin_relu2_kernel(tc, x_words, x_scales, w, offs, out):
             both = y[:, first:first + HALVES, :]
             nc.scalar.activation(out=both, in_=both, func=ACT.Square)
             if e == start + count - 1:
-                nc.sync.dma_start(
-                    out=out[start * C:(e + 1) * C, :].rearrange("(h p) n -> p h n", p=P),
-                    in_=y[:],
-                )
+                rows = out[start * C:(e + 1) * C, :].rearrange("(h p) n -> p h n", p=P)
+                if g > 0:
+                    nc.sync.dma_start(out=rows, in_=y[:])
+                    return
+                nc.sync.dma_start(out=rows[:, 1:, :], in_=y[:, 1:, :])
+                for low, high in LOW_ENGINES:
+                    nc.sync.dma_start(out=rows[low:high, 0, :], in_=y[low:high, 0, :])
 
         done = None
         for e in range(E - 1):

@@ -27,7 +27,7 @@ SLOT = PACK * N * 4
 SCALAR_PASSES = 7
 LOADS = [1, 1, 2, 2, 2, 2, 2, 1, 1, 1, 1]
 STORES = [4, 2, 1]
-LOW_ENGINES = [(0, 44), (44, 88), (88, 128)]
+LOW_ENGINES = [(0, 60), (60, 100), (100, 128)]
 
 
 def tile_moe_s_lin_relu2_kernel(tc, x_words, x_scales, w, offs, out):

@@ -143,7 +143,7 @@ def tile_moe_s_lin_relu2_kernel(tc, x_words, x_scales, w, offs, out):
             nc.scalar.activation(out=both, in_=both, func=ACT.Square)
             if e == start + count - 1:
                 rows = out[start * C:(e + 1) * C, :].rearrange("(h p) n -> p h n", p=P)
-                if g > 0:
+                if g < len(STORES) - 1:
                     nc.sync.dma_start(out=rows, in_=y[:])
                     return
                 nc.sync.dma_start(out=rows[:, 1:, :], in_=y[:, 1:, :])

@@ -17,17 +17,19 @@ ACT = mybir.ActivationFunctionType
 
 P = 128
 PACK = 4
-K_PASS = P * PACK
-PASSES = K // K_PASS
+PASSES = K // (P * PACK)
+SLOTS = E * C
 HALVES = C // P
 RUN = 4
-CUT = 512
 ALIGN = 256
-SLOT = PACK * N * 4
+RAW = PACK * N * 4
+ROUNDED = RAW // 2
+WORD_CUT = 768
+BYTE_CUT = 1024
+BYTE_WINDOW = 1536
 SCALAR_PASSES = 7
 LOADS = [1, 1, 2, 2, 2, 2, 2, 1, 1, 1, 1]
-STORES = [4, 2, 1]
-LOW_ENGINES = [(0, 60), (60, 100), (100, 128)]
+STORES = [4, 2, 1, 1]
 
 
 def tile_moe_s_lin_relu2_kernel(tc, x_words, x_scales, w, offs, out):
@@ -35,149 +37,149 @@ def tile_moe_s_lin_relu2_kernel(tc, x_words, x_scales, w, offs, out):
     with ExitStack() as ctx:
         keep = ctx.enter_context(tc.tile_pool(name="keep", bufs=1))
         big = ctx.enter_context(tc.tile_pool(name="big", bufs=1))
-        ring = ctx.enter_context(tc.tile_pool(name="ring", bufs=E * PASSES))
         psum = ctx.enter_context(tc.psum_pool(name="psum", bufs=8))
 
-        offsets = keep.tile([P, E * C // 16], U16, name="offsets", align_bytes=ALIGN)
+        offsets = keep.tile([P, SLOTS // 16], U16, name="offsets", align_bytes=ALIGN)
         words = keep.tile([P, T], I32, name="words", align_bytes=ALIGN)
-        scales = keep.tile([P, PASSES * T // 4], I32, name="scales", align_bytes=ALIGN)
-        x_scale = [keep.tile([P, E * C], U8, name="x_scale%d" % s, align_bytes=ALIGN) for s in range(PASSES)]
+        scales = keep.tile([P, (T + BYTE_WINDOW) // 4], I32, name="scales", align_bytes=ALIGN)
 
         nc.vector.memset(scales[:], 0)
         nc.sync.dma_start(out=words[:], in_=x_words[0].rearrange("p t d -> p (t d)").bitcast(I32))
         nc.sync.dma_start(offsets[:], offs)
 
         rows_k = w.rearrange("e (s p j) n -> p (e s) j n", p=P, j=PACK)
-        raw = {}
-        first_pass = 0
+        loaded = []
+        first = 0
         for count in LOADS:
-            part = big.tile([P, count, PACK, N], F32, name="raw%d" % first_pass, align_bytes=ALIGN, offset=first_pass * SLOT)
-            nc.sync.dma_start(out=part[:], in_=rows_k[:, first_pass:first_pass + count])
-            if first_pass == 0:
+            raw = big.tile([P, count, PACK, N], F32, name="raw%d" % first, align_bytes=ALIGN, offset=first * RAW)
+            nc.sync.dma_start(out=raw[:], in_=rows_k[:, first:first + count])
+            if first == 0:
                 for r in range(4):
                     nc.sync.dma_start(
-                        out=scales[r:P:32, :].rearrange("q (s t) -> q s t", s=PASSES),
+                        out=scales[r:P:32, :PASSES * T // 4].rearrange("q (s t) -> q s t", s=PASSES),
                         in_=x_scales[:, r:16:4, :].bitcast(I32).rearrange("s q t -> q s t"),
                     )
-            for i in range(count):
-                raw[first_pass + i] = part[:, i]
-            first_pass = first_pass + count
+            loaded.append((first, count, raw))
+            first = first + count
 
-        paired = keep.tile([P, E * C], U32, name="paired", align_bytes=ALIGN)
-        x_code = keep.tile([P, PASSES, 2 * E * C], U8, name="x_code", align_bytes=ALIGN)
-        for c in range(E * C // CUT):
-            slots = offsets[:, c * CUT // 16:(c + 1) * CUT // 16]
-            nc.vector.tensor_copy(out=paired[:, c * CUT:(c + 1) * CUT], in_=words[:].bitcast(U32).indirect(slots))
-        for c in range(E * C // CUT):
-            nc.vector.tensor_copy(
-                out=x_code[:, :, 2 * c * CUT:2 * (c + 1) * CUT].bitcast(U16),
-                in_=paired[:, c * CUT:(c + 1) * CUT].bitcast(U16).rearrange("p (u s) -> p s u", s=PASSES),
-            )
-        for c in range(E * C // CUT):
-            slots = offsets[:, c * CUT // 16:(c + 1) * CUT // 16]
+        def listed(low, high):
+            return offsets[:, low // 16:high // 16]
+
+        paired = keep.tile([P, SLOTS], U32, name="paired", align_bytes=ALIGN)
+        for low in range(0, SLOTS, WORD_CUT):
+            high = min(low + WORD_CUT, SLOTS)
+            nc.vector.tensor_copy(out=paired[:, low:high], in_=words[:].bitcast(U32).indirect(listed(low, high)))
+        x_code = keep.tile([P, PASSES, 2 * SLOTS], U8, name="x_code", align_bytes=ALIGN)
+        nc.vector.tensor_copy(
+            out=x_code[:].bitcast(U16),
+            in_=paired[:].bitcast(U16).rearrange("p (u s) -> p s u", s=PASSES),
+        )
+        x_scale = [keep.tile([P, SLOTS], U8, name="x_scale%d" % s, align_bytes=ALIGN) for s in range(PASSES)]
+        for low in range(0, SLOTS, BYTE_CUT):
             for s in range(PASSES):
-                window = scales[:].bitcast(U8)[:, s * T:(s + 1) * T]
-                nc.vector.tensor_copy(out=x_scale[s][:, c * CUT:(c + 1) * CUT], in_=window.indirect(slots))
+                window = scales[:].bitcast(U8)[:, s * T:s * T + BYTE_WINDOW]
+                nc.vector.tensor_copy(
+                    out=x_scale[s][:, low:low + BYTE_CUT],
+                    in_=window.indirect(listed(low, low + BYTE_CUT)),
+                )
 
-        def views(g, i, cols):
-            dst = g.rearrange("p (c i) t -> p c t i", i=RUN)
-            src = raw[i][:, :, cols].rearrange("p t (c i) -> p c t i", i=RUN)
+        def rounded_tile(first, count):
+            place = first % E
+            return big.tile(
+                [P, count, N, PACK], BF16, name="rounded%d" % first, align_bytes=ALIGN,
+                offset=E * PASSES * RAW + place * ROUNDED,
+            )
+
+        def views(rounded, raw):
+            dst = rounded.rearrange("p a (c i) t -> p a c t i", i=RUN)
+            src = raw.rearrange("p a t (c i) -> p a c t i", i=RUN)
             return dst, src
 
-        def quantise(code, scale, cols, g):
-            nc.vector.quantize_mx(
-                out=code[:, cols].bitcast(FP8X4),
-                scales=scale[:, cols],
-                in_=g[:].rearrange("p n t -> p (n t)"),
-            )
+        def parts(first, count):
+            if first < SCALAR_PASSES:
+                return [(slice(0, count), slice(0, N))]
+            if count == 2:
+                return [(slice(a, a + 1), slice(0, N)) for a in range(count)]
+            return [(slice(0, 1), slice(u * N // 2, (u + 1) * N // 2)) for u in range(2)]
 
-        def quantised(i):
-            code = ring.tile([P, N], U32, name="w_code", align_bytes=ALIGN)
-            scale = ring.tile([P, N], U8, name="w_scale", align_bytes=ALIGN)
-            if i < SCALAR_PASSES:
-                g = keep.tile([P, N, PACK], BF16, name="grouped%d" % i, align_bytes=ALIGN)
-                dst, src = views(g[:], i, slice(0, N))
-                nc.scalar.activation(out=dst, in_=src, func=ACT.Copy)
-                parts = [(slice(0, N), g)]
-            else:
-                parts = []
-                for u in range(2):
-                    g = big.tile([P, N // 2, PACK], BF16, name="grouped%d_%d" % (i, u), align_bytes=ALIGN, offset=E * PASSES * SLOT + u * SLOT // 4)
-                    parts.append((slice(u * N // 2, (u + 1) * N // 2), g))
-                for cols, g in parts:
-                    dst, src = views(g[:], i, cols)
+        def quantised(first, count, raw):
+            rounded = rounded_tile(first, count)
+            code = keep.tile([P, count, N], U32, name="w_code%d" % first, align_bytes=ALIGN)
+            scale = keep.tile([P, count, N], U8, name="w_scale%d" % first, align_bytes=ALIGN)
+            shared = min(max(SCALAR_PASSES - first, 0), count)
+            for a in range(shared):
+                dst, src = views(rounded[:, a:a + 1], raw[:, a:a + 1])
+                nc.scalar.activation(out=dst[:, 0], in_=src[:, 0], func=ACT.Copy)
+            for passes, cols in parts(first, count):
+                if shared < count:
+                    mine = slice(max(passes.start, shared), passes.stop)
+                    dst, src = views(rounded[:, mine, cols, :], raw[:, mine, :, cols])
                     nc.vector.tensor_copy(out=dst, in_=src)
-            for cols, g in parts:
-                quantise(code, scale, cols, g)
-            return code, scale
+            for passes, cols in parts(first, count):
+                nc.vector.quantize_mx(
+                    out=code[:, passes, cols].rearrange("p a n -> p (a n)").bitcast(FP8X4),
+                    scales=scale[:, passes, cols].rearrange("p a n -> p (a n)"),
+                    in_=rounded[:, passes, cols, :].rearrange("p a n t -> p (a n t)"),
+                )
+            return [(code[:, a], scale[:, a]) for a in range(count)]
 
-        def multiply(acc, e, s, h, code, scale, cols):
+        def multiply(acc, e, s, h, code, scale):
+            low = C * e + P * h
             nc.tensor.matmul_mx(
                 out=acc[:],
-                lhsT=x_code[:, s, 2 * (C * e + P * h):2 * (C * e + P * (h + 1))].bitcast(FP4X4),
-                lhsT_scale=x_scale[s][:, C * e + P * h:C * e + P * (h + 1)],
-                rhs=code[:, cols].bitcast(FP8X4),
-                rhs_scale=scale[:, cols],
+                lhsT=x_code[:, s, 2 * low:2 * (low + P)].bitcast(FP4X4),
+                lhsT_scale=x_scale[s][:, low:low + P],
+                rhs=code.bitcast(FP8X4),
+                rhs_scale=scale,
                 start=(s == 0),
                 stop=(s == PASSES - 1),
             )
 
-        group = {}
-        first_expert = 0
-        for g, count in enumerate(STORES):
-            for e in range(first_expert, first_expert + count):
-                group[e] = (g, first_expert, count)
-            first_expert = first_expert + count
-        places = [6 * SLOT, 0, SLOT, SLOT + SLOT // 2]
-        results = {}
+        places = [(SCALAR_PASSES - 1) * RAW, 0, RAW, RAW + RAW // 2]
+        stores = []
+        first = 0
+        for count, place in zip(STORES, places):
+            y = big.tile([P, count * HALVES, N], F32, name="y%d" % first, align_bytes=ALIGN, offset=place)
+            stores.extend([(first, count, y)] * count)
+            first = first + count
+
+        def store(e):
+            first, count, y = stores[e]
+            nc.sync.dma_start(out=out[first * C:(e + 1) * C, :].rearrange("(h p) n -> p h n", p=P), in_=y[:])
 
         def finish(e, acc):
-            g, start, count = group[e]
-            if e == start:
-                results[g] = big.tile([P, count * HALVES, N], F32, name="y%d" % e, align_bytes=ALIGN, offset=places[g])
-            y = results[g]
-            first = (e - start) * HALVES
+            first, count, y = stores[e]
             for h in range(HALVES):
-                nc.scalar.activation(out=y[:, first + h, :], in_=acc[h][:], func=ACT.Relu)
-            both = y[:, first:first + HALVES, :]
-            nc.scalar.activation(out=both, in_=both, func=ACT.Square)
-            if e == start + count - 1:
-                rows = out[start * C:(e + 1) * C, :].rearrange("(h p) n -> p h n", p=P)
-                if g < len(STORES) - 1:
-                    nc.sync.dma_start(out=rows, in_=y[:])
-                    return
-                nc.sync.dma_start(out=rows[:, 1:, :], in_=y[:, 1:, :])
-                for low, high in LOW_ENGINES:
-                    nc.sync.dma_start(out=rows[low:high, 0, :], in_=y[low:high, 0, :])
+                nc.scalar.activation(out=y[:, (e - first) * HALVES + h, :], in_=acc[h][:], func=ACT.Relu)
+            if e == first + count - 1:
+                nc.scalar.activation(out=y[:], in_=y[:], func=ACT.Square)
+                store(e)
 
-        done = None
-        for e in range(E - 1):
-            acc = [psum.tile([P, N], F32, name="acc") for h in range(HALVES)]
-            for s in range(PASSES):
-                code, scale = quantised(PASSES * e + s)
-                if s == 0 and e > 0:
-                    finish(e - 1, done)
-                for h in range(HALVES):
-                    multiply(acc[h], e, s, h, code, scale, slice(0, N))
-            done = acc
+        acc = {}
+        for first, count, raw in loaded:
+            for a, (code, scale) in enumerate(quantised(first, count, raw)):
+                e, s = divmod(first + a, PASSES)
+                if e < E - 1:
+                    if s == 0:
+                        acc = [psum.tile([P, N], F32, name="acc") for h in range(HALVES)]
+                    for h in range(HALVES):
+                        multiply(acc[h], e, s, h, code, scale)
+                    if s == PASSES - 1:
+                        finish(e, acc)
+                    continue
+                if s == 0:
+                    acc = {(u, h): psum.tile([P, N // 2], F32, name="acc") for u in range(2) for h in range(HALVES)}
+                for u in range(2):
+                    cols = slice(u * N // 2, (u + 1) * N // 2)
+                    for h in range(HALVES):
+                        multiply(acc[u, h], e, s, h, code[:, cols], scale[:, cols])
 
-        e = E - 1
-        order = [(u, h, b) for u in range(2) for h in range(HALVES) for b in range(2)]
-        acc = {key: psum.tile([P, P], F32, name="acc") for key in order}
-        for s in range(PASSES):
-            code, scale = quantised(PASSES * e + s)
-            if s == 0:
-                finish(e - 1, done)
-            for u, h, b in order:
-                multiply(acc[u, h, b], e, s, h, code, scale, slice((2 * u + b) * P, (2 * u + b + 1) * P))
-        y = big.tile([P, HALVES, N], F32, name="y_last", align_bytes=ALIGN, offset=places[-1])
+        y = stores[E - 1][2]
         positive = keep.tile([P, N], F32, name="positive")
         for u in range(2):
             cols = slice(u * N // 2, (u + 1) * N // 2)
-            for b in range(2):
-                block = slice((2 * u + b) * P, (2 * u + b + 1) * P)
-                nc.scalar.activation(out=y[:, 0, block], in_=acc[u, 0, b][:], func=ACT.Relu)
-                nc.vector.tensor_scalar_max(positive[:, block], acc[u, 1, b][:], 0.0)
-            nc.scalar.activation(out=y[:, 0, cols], in_=y[:, 0, cols], func=ACT.Square)
-            nc.vector.tensor_tensor(y[:, 1, cols], positive[:, cols], positive[:, cols], mybir.AluOpType.mult)
-        nc.sync.dma_start(out=out[e * C:(e + 1) * C, :].rearrange("(h p) n -> p h n", p=P), in_=y[:])
+            nc.scalar.activation(out=y[:, 0, cols], in_=acc[u, 0][:], func=ACT.Relu)
+            nc.vector.tensor_scalar_max(positive[:, cols], acc[u, 1][:], 0.0)
+        nc.scalar.activation(out=y[:, 0, :], in_=y[:, 0, :], func=ACT.Square)
+        nc.vector.tensor_tensor(y[:, 1, :], positive[:], positive[:], mybir.AluOpType.mult)
+        store(E - 1)

@@ -30,6 +30,8 @@ BYTE_WINDOW = 1536
 SCALAR_PASSES = 7
 LOADS = [1, 1, 2, 2, 2, 2, 2, 1, 1, 1, 1]
 STORES = [4, 2, 1, 1]
+SHIFTED = E - 2
+LOW = 112
 
 
 def tile_moe_s_lin_relu2_kernel(tc, x_words, x_scales, w, offs, out):
@@ -145,7 +147,13 @@ def tile_moe_s_lin_relu2_kernel(tc, x_words, x_scales, w, offs, out):
 
         def store(e):
             first, count, y = stores[e]
-            nc.sync.dma_start(out=out[first * C:(e + 1) * C, :].rearrange("(h p) n -> p h n", p=P), in_=y[:])
+            rows = out[first * C:(e + 1) * C, :].rearrange("(h p) n -> p h n", p=P)
+            if e != SHIFTED:
+                nc.sync.dma_start(out=rows, in_=y[:])
+                return
+            nc.sync.dma_start(out=rows[:LOW, 0, :], in_=y[:LOW, 0, :])
+            nc.sync.dma_start(out=rows[LOW:, 0, :], in_=y[LOW:, 0, :])
+            nc.sync.dma_start(out=rows[:, 1, :], in_=y[:, 1, :])
 
         def finish(e, acc):
             first, count, y = stores[e]

@@ -31,7 +31,7 @@ SCALAR_PASSES = 7
 LOADS = [1, 1, 2, 2, 2, 2, 2, 1, 1, 1, 1]
 STORES = [4, 2, 1, 1]
 SHIFTED = E - 2
-LOW = 112
+LOW = 98
 
 
 def tile_moe_s_lin_relu2_kernel(tc, x_words, x_scales, w, offs, out):
@@ -188,6 +188,6 @@ def tile_moe_s_lin_relu2_kernel(tc, x_words, x_scales, w, offs, out):
             cols = slice(u * N // 2, (u + 1) * N // 2)
             nc.scalar.activation(out=y[:, 0, cols], in_=acc[u, 0][:], func=ACT.Relu)
             nc.vector.tensor_scalar_max(positive[:, cols], acc[u, 1][:], 0.0)
-        nc.scalar.activation(out=y[:, 0, :], in_=y[:, 0, :], func=ACT.Square)
-        nc.vector.tensor_tensor(y[:, 1, :], positive[:], positive[:], mybir.AluOpType.mult)
+            nc.scalar.activation(out=y[:, 0, cols], in_=y[:, 0, cols], func=ACT.Square)
+            nc.vector.tensor_tensor(y[:, 1, cols], positive[:, cols], positive[:, cols], mybir.AluOpType.mult)
         store(E - 1)

@@ -31,7 +31,7 @@ SCALAR_PASSES = 7
 LOADS = [1, 1, 2, 2, 2, 2, 2, 1, 1, 1, 1]
 STORES = [4, 2, 1, 1]
 SHIFTED = E - 2
-LOW = 98
+LOW = 120
 
 
 def tile_moe_s_lin_relu2_kernel(tc, x_words, x_scales, w, offs, out):

@@ -28,9 +28,9 @@ WORD_CUT = 768
 BYTE_CUT = 1024
 BYTE_WINDOW = 1536
 SCALAR_PASSES = 7
-LOADS = [1, 1, 2, 2, 2, 2, 2, 1, 1, 1, 1]
-STORES = [4, 2, 1, 1]
-SHIFTED = E - 2
+LOADS = [2, 2, 2, 2, 2, 2, 1, 1, 1, 1]
+STORES = [5, 2, 1]
+SQUARED = [1, 3, 4, 5, 6]
 LOW = 120
 
 
@@ -137,7 +137,7 @@ def tile_moe_s_lin_relu2_kernel(tc, x_words, x_scales, w, offs, out):
                 stop=(s == PASSES - 1),
             )
 
-        places = [(SCALAR_PASSES - 1) * RAW, 0, RAW, RAW + RAW // 2]
+        places = [(SCALAR_PASSES - 1) * RAW - RAW // 2, 0, RAW]
         stores = []
         first = 0
         for count, place in zip(STORES, places):
@@ -148,19 +148,22 @@ def tile_moe_s_lin_relu2_kernel(tc, x_words, x_scales, w, offs, out):
         def store(e):
             first, count, y = stores[e]
             rows = out[first * C:(e + 1) * C, :].rearrange("(h p) n -> p h n", p=P)
-            if e != SHIFTED:
+            if first > 0:
                 nc.sync.dma_start(out=rows, in_=y[:])
                 return
             nc.sync.dma_start(out=rows[:LOW, 0, :], in_=y[:LOW, 0, :])
             nc.sync.dma_start(out=rows[LOW:, 0, :], in_=y[LOW:, 0, :])
-            nc.sync.dma_start(out=rows[:, 1, :], in_=y[:, 1, :])
+            nc.sync.dma_start(out=rows[:, 1:, :], in_=y[:, 1:, :])
 
         def finish(e, acc):
             first, count, y = stores[e]
             for h in range(HALVES):
                 nc.scalar.activation(out=y[:, (e - first) * HALVES + h, :], in_=acc[h][:], func=ACT.Relu)
+            if e in SQUARED:
+                since = max([0] + [d + 1 for d in SQUARED if d < e])
+                part = y[:, (since - first) * HALVES:(e + 1 - first) * HALVES, :]
+                nc.scalar.activation(out=part, in_=part, func=ACT.Square)
             if e == first + count - 1:
-                nc.scalar.activation(out=y[:], in_=y[:], func=ACT.Square)
                 store(e)
 
         acc = {}

@@ -30,7 +30,6 @@ BYTE_WINDOW = 1536
 SCALAR_PASSES = 7
 LOADS = [2, 2, 2, 2, 2, 2, 1, 1, 1, 1]
 STORES = [5, 2, 1]
-SQUARED = [1, 3, 4, 5, 6]
 LOW = 120
 
 
@@ -137,11 +136,12 @@ def tile_moe_s_lin_relu2_kernel(tc, x_words, x_scales, w, offs, out):
                 stop=(s == PASSES - 1),
             )
 
-        places = [(SCALAR_PASSES - 1) * RAW - RAW // 2, 0, RAW]
+        first, count, raw = [load for load in loaded if load[0] < SCALAR_PASSES][-1]
+        clipped = raw[:, SCALAR_PASSES - 1 - first, :HALVES, :]
         stores = []
         first = 0
-        for count, place in zip(STORES, places):
-            y = big.tile([P, count * HALVES, N], F32, name="y%d" % first, align_bytes=ALIGN, offset=place)
+        for count in STORES:
+            y = big.tile([P, count * HALVES, N], F32, name="y%d" % first, align_bytes=ALIGN, offset=first * RAW // 2)
             stores.extend([(first, count, y)] * count)
             first = first + count
 
@@ -158,15 +158,14 @@ def tile_moe_s_lin_relu2_kernel(tc, x_words, x_scales, w, offs, out):
         def finish(e, acc):
             first, count, y = stores[e]
             for h in range(HALVES):
-                nc.scalar.activation(out=y[:, (e - first) * HALVES + h, :], in_=acc[h][:], func=ACT.Relu)
-            if e in SQUARED:
-                since = max([0] + [d + 1 for d in SQUARED if d < e])
-                part = y[:, (since - first) * HALVES:(e + 1 - first) * HALVES, :]
-                nc.scalar.activation(out=part, in_=part, func=ACT.Square)
+                nc.scalar.activation(out=clipped[:, h, :], in_=acc[h][:], func=ACT.Relu)
+            for h in range(HALVES):
+                nc.scalar.activation(out=y[:, (e - first) * HALVES + h, :], in_=clipped[:, h, :], func=ACT.Square)
             if e == first + count - 1:
                 store(e)
 
         acc = {}
+        waiting = []
         for first, count, raw in loaded:
             for a, (code, scale) in enumerate(quantised(first, count, raw)):
                 e, s = divmod(first + a, PASSES)
@@ -176,7 +175,11 @@ def tile_moe_s_lin_relu2_kernel(tc, x_words, x_scales, w, offs, out):
                     for h in range(HALVES):
                         multiply(acc[h], e, s, h, code, scale)
                     if s == PASSES - 1:
-                        finish(e, acc)
+                        waiting.append((e, acc))
+                    if first + count >= SCALAR_PASSES:
+                        for done in waiting:
+                            finish(*done)
+                        waiting.clear()
                     continue
                 if s == 0:
                     acc = {(u, h): psum.tile([P, N // 2], F32, name="acc") for u in range(2) for h in range(HALVES)}
@@ -189,8 +192,8 @@ def tile_moe_s_lin_relu2_kernel(tc, x_words, x_scales, w, offs, out):
         positive = keep.tile([P, N], F32, name="positive")
         for u in range(2):
             cols = slice(u * N // 2, (u + 1) * N // 2)
-            nc.scalar.activation(out=y[:, 0, cols], in_=acc[u, 0][:], func=ACT.Relu)
+            nc.scalar.activation(out=clipped[:, 0, cols], in_=acc[u, 0][:], func=ACT.Relu)
             nc.vector.tensor_scalar_max(positive[:, cols], acc[u, 1][:], 0.0)
-            nc.scalar.activation(out=y[:, 0, cols], in_=y[:, 0, cols], func=ACT.Square)
+            nc.scalar.activation(out=y[:, 0, cols], in_=clipped[:, 0, cols], func=ACT.Square)
             nc.vector.tensor_tensor(y[:, 1, cols], positive[:, cols], positive[:, cols], mybir.AluOpType.mult)
         store(E - 1)

@@ -1,3 +1,4 @@
+import itertools
 from contextlib import ExitStack
 
 import concourse.mybir as mybir
@@ -29,7 +30,7 @@ BYTE_CUT = 1024
 BYTE_WINDOW = 1536
 SCALAR_PASSES = 7
 LOADS = [2, 2, 2, 2, 2, 2, 1, 1, 1, 1]
-STORES = [5, 2, 1]
+STORES = [8, 1, 4, 3]
 LOW = 120
 
 
@@ -138,31 +139,26 @@ def tile_moe_s_lin_relu2_kernel(tc, x_words, x_scales, w, offs, out):
 
         first, count, raw = [load for load in loaded if load[0] < SCALAR_PASSES][-1]
         clipped = raw[:, SCALAR_PASSES - 1 - first, :HALVES, :]
-        stores = []
-        first = 0
-        for count in STORES:
-            y = big.tile([P, count * HALVES, N], F32, name="y%d" % first, align_bytes=ALIGN, offset=first * RAW // 2)
-            stores.extend([(first, count, y)] * count)
-            first = first + count
+        y = big.tile([P, E * HALVES, N], F32, name="y", align_bytes=ALIGN, offset=0)
+        rows = out.rearrange("(h p) n -> p h n", p=P)
+        ends = list(itertools.accumulate(STORES))
 
         def store(e):
-            first, count, y = stores[e]
-            rows = out[first * C:(e + 1) * C, :].rearrange("(h p) n -> p h n", p=P)
-            if first > 0:
-                nc.sync.dma_start(out=rows, in_=y[:])
-                return
-            nc.sync.dma_start(out=rows[:LOW, 0, :], in_=y[:LOW, 0, :])
-            nc.sync.dma_start(out=rows[LOW:, 0, :], in_=y[LOW:, 0, :])
-            nc.sync.dma_start(out=rows[:, 1:, :], in_=y[:, 1:, :])
+            for count, end in zip(STORES, ends):
+                if (end - 1) // HALVES != e:
+                    continue
+                if count == 1:
+                    nc.sync.dma_start(out=rows[:LOW, end - 1, :], in_=y[:LOW, end - 1, :])
+                    nc.sync.dma_start(out=rows[LOW:, end - 1, :], in_=y[LOW:, end - 1, :])
+                else:
+                    nc.sync.dma_start(out=rows[:, end - count:end, :], in_=y[:, end - count:end, :])
 
         def finish(e, acc):
-            first, count, y = stores[e]
             for h in range(HALVES):
                 nc.scalar.activation(out=clipped[:, h, :], in_=acc[h][:], func=ACT.Relu)
             for h in range(HALVES):
-                nc.scalar.activation(out=y[:, (e - first) * HALVES + h, :], in_=clipped[:, h, :], func=ACT.Square)
-            if e == first + count - 1:
-                store(e)
+                nc.scalar.activation(out=y[:, e * HALVES + h, :], in_=clipped[:, h, :], func=ACT.Square)
+            store(e)
 
         acc = {}
         waiting = []
@@ -188,12 +184,12 @@ def tile_moe_s_lin_relu2_kernel(tc, x_words, x_scales, w, offs, out):
                     for h in range(HALVES):
                         multiply(acc[u, h], e, s, h, code[:, cols], scale[:, cols])
 
-        y = stores[E - 1][2]
+        last = (E - 1) * HALVES
         positive = keep.tile([P, N], F32, name="positive")
         for u in range(2):
             cols = slice(u * N // 2, (u + 1) * N // 2)
             nc.scalar.activation(out=clipped[:, 0, cols], in_=acc[u, 0][:], func=ACT.Relu)
             nc.vector.tensor_scalar_max(positive[:, cols], acc[u, 1][:], 0.0)
-            nc.scalar.activation(out=y[:, 0, cols], in_=clipped[:, 0, cols], func=ACT.Square)
-            nc.vector.tensor_tensor(y[:, 1, cols], positive[:, cols], positive[:, cols], mybir.AluOpType.mult)
+            nc.scalar.activation(out=y[:, last, cols], in_=clipped[:, 0, cols], func=ACT.Square)
+            nc.vector.tensor_tensor(y[:, last + 1, cols], positive[:, cols], positive[:, cols], mybir.AluOpType.mult)
         store(E - 1)

@@ -29,7 +29,7 @@ WORD_CUT = 768
 BYTE_CUT = 1024
 BYTE_WINDOW = 1536
 SCALAR_PASSES = 7
-LOADS = [2, 2, 2, 2, 2, 2, 1, 1, 1, 1]
+LOADS = [1, 1, 2, 2, 2, 2, 2, 1, 1, 1, 1]
 STORES = [8, 1, 4, 3]
 LOW = 120
 

import itertools
from contextlib import ExitStack

import concourse.mybir as mybir

K, T, E, C, N = 1024, 1024, 8, 256, 512
FLOPS = 2 * E * C * K * N

F32 = mybir.dt.float32
BF16 = mybir.dt.bfloat16
I32 = mybir.dt.int32
U32 = mybir.dt.uint32
U16 = mybir.dt.uint16
U8 = mybir.dt.uint8
FP8X4 = mybir.dt.float8_e4m3fn_x4
FP4X4 = mybir.dt.float4_e2m1fn_x4
ACT = mybir.ActivationFunctionType

P = 128
PACK = 4
PASSES = K // (P * PACK)
SLOTS = E * C
HALVES = C // P
RUN = 4
ALIGN = 256
RAW = PACK * N * 4
ROUNDED = RAW // 2
WORD_CUT = 768
BYTE_CUT = 1024
BYTE_WINDOW = 1536
SCALAR_PASSES = 7
LOADS = [1, 1, 2, 2, 2, 2, 2, 1, 1, 1, 1]
STORES = [8, 1, 4, 3]
LOW = 120


def tile_moe_s_lin_relu2_kernel(tc, x_words, x_scales, w, offs, out):
    nc = tc.nc
    with ExitStack() as ctx:
        keep = ctx.enter_context(tc.tile_pool(name="keep", bufs=1))
        big = ctx.enter_context(tc.tile_pool(name="big", bufs=1))
        psum = ctx.enter_context(tc.psum_pool(name="psum", bufs=8))

        offsets = keep.tile([P, SLOTS // 16], U16, name="offsets", align_bytes=ALIGN)
        words = keep.tile([P, T], I32, name="words", align_bytes=ALIGN)
        scales = keep.tile([P, (T + BYTE_WINDOW) // 4], I32, name="scales", align_bytes=ALIGN)

        nc.vector.memset(scales[:], 0)
        nc.sync.dma_start(out=words[:], in_=x_words[0].rearrange("p t d -> p (t d)").bitcast(I32))
        nc.sync.dma_start(offsets[:], offs)

        rows_k = w.rearrange("e (s p j) n -> p (e s) j n", p=P, j=PACK)
        loaded = []
        first = 0
        for count in LOADS:
            raw = big.tile([P, count, PACK, N], F32, name="raw%d" % first, align_bytes=ALIGN, offset=first * RAW)
            nc.sync.dma_start(out=raw[:], in_=rows_k[:, first:first + count])
            if first == 0:
                for r in range(4):
                    nc.sync.dma_start(
                        out=scales[r:P:32, :PASSES * T // 4].rearrange("q (s t) -> q s t", s=PASSES),
                        in_=x_scales[:, r:16:4, :].bitcast(I32).rearrange("s q t -> q s t"),
                    )
            loaded.append((first, count, raw))
            first = first + count

        def listed(low, high):
            return offsets[:, low // 16:high // 16]

        paired = keep.tile([P, SLOTS], U32, name="paired", align_bytes=ALIGN)
        for low in range(0, SLOTS, WORD_CUT):
            high = min(low + WORD_CUT, SLOTS)
            nc.vector.tensor_copy(out=paired[:, low:high], in_=words[:].bitcast(U32).indirect(listed(low, high)))
        x_code = keep.tile([P, PASSES, 2 * SLOTS], U8, name="x_code", align_bytes=ALIGN)
        nc.vector.tensor_copy(
            out=x_code[:].bitcast(U16),
            in_=paired[:].bitcast(U16).rearrange("p (u s) -> p s u", s=PASSES),
        )
        x_scale = [keep.tile([P, SLOTS], U8, name="x_scale%d" % s, align_bytes=ALIGN) for s in range(PASSES)]
        for low in range(0, SLOTS, BYTE_CUT):
            for s in range(PASSES):
                window = scales[:].bitcast(U8)[:, s * T:s * T + BYTE_WINDOW]
                nc.vector.tensor_copy(
                    out=x_scale[s][:, low:low + BYTE_CUT],
                    in_=window.indirect(listed(low, low + BYTE_CUT)),
                )

        def rounded_tile(first, count):
            place = first % E
            return big.tile(
                [P, count, N, PACK], BF16, name="rounded%d" % first, align_bytes=ALIGN,
                offset=E * PASSES * RAW + place * ROUNDED,
            )

        def views(rounded, raw):
            dst = rounded.rearrange("p a (c i) t -> p a c t i", i=RUN)
            src = raw.rearrange("p a t (c i) -> p a c t i", i=RUN)
            return dst, src

        def parts(first, count):
            if first < SCALAR_PASSES:
                return [(slice(0, count), slice(0, N))]
            if count == 2:
                return [(slice(a, a + 1), slice(0, N)) for a in range(count)]
            return [(slice(0, 1), slice(u * N // 2, (u + 1) * N // 2)) for u in range(2)]

        def quantised(first, count, raw):
            rounded = rounded_tile(first, count)
            code = keep.tile([P, count, N], U32, name="w_code%d" % first, align_bytes=ALIGN)
            scale = keep.tile([P, count, N], U8, name="w_scale%d" % first, align_bytes=ALIGN)
            shared = min(max(SCALAR_PASSES - first, 0), count)
            for a in range(shared):
                dst, src = views(rounded[:, a:a + 1], raw[:, a:a + 1])
                nc.scalar.activation(out=dst[:, 0], in_=src[:, 0], func=ACT.Copy)
            for passes, cols in parts(first, count):
                if shared < count:
                    mine = slice(max(passes.start, shared), passes.stop)
                    dst, src = views(rounded[:, mine, cols, :], raw[:, mine, :, cols])
                    nc.vector.tensor_copy(out=dst, in_=src)
            for passes, cols in parts(first, count):
                nc.vector.quantize_mx(
                    out=code[:, passes, cols].rearrange("p a n -> p (a n)").bitcast(FP8X4),
                    scales=scale[:, passes, cols].rearrange("p a n -> p (a n)"),
                    in_=rounded[:, passes, cols, :].rearrange("p a n t -> p (a n t)"),
                )
            return [(code[:, a], scale[:, a]) for a in range(count)]

        def multiply(acc, e, s, h, code, scale):
            low = C * e + P * h
            nc.tensor.matmul_mx(
                out=acc[:],
                lhsT=x_code[:, s, 2 * low:2 * (low + P)].bitcast(FP4X4),
                lhsT_scale=x_scale[s][:, low:low + P],
                rhs=code.bitcast(FP8X4),
                rhs_scale=scale,
                start=(s == 0),
                stop=(s == PASSES - 1),
            )

        first, count, raw = [load for load in loaded if load[0] < SCALAR_PASSES][-1]
        clipped = raw[:, SCALAR_PASSES - 1 - first, :HALVES, :]
        y = big.tile([P, E * HALVES, N], F32, name="y", align_bytes=ALIGN, offset=0)
        rows = out.rearrange("(h p) n -> p h n", p=P)
        ends = list(itertools.accumulate(STORES))

        def store(e):
            for count, end in zip(STORES, ends):
                if (end - 1) // HALVES != e:
                    continue
                if count == 1:
                    nc.sync.dma_start(out=rows[:LOW, end - 1, :], in_=y[:LOW, end - 1, :])
                    nc.sync.dma_start(out=rows[LOW:, end - 1, :], in_=y[LOW:, end - 1, :])
                else:
                    nc.sync.dma_start(out=rows[:, end - count:end, :], in_=y[:, end - count:end, :])

        def finish(e, acc):
            for h in range(HALVES):
                nc.scalar.activation(out=clipped[:, h, :], in_=acc[h][:], func=ACT.Relu)
            for h in range(HALVES):
                nc.scalar.activation(out=y[:, e * HALVES + h, :], in_=clipped[:, h, :], func=ACT.Square)
            store(e)

        acc = {}
        waiting = []
        for first, count, raw in loaded:
            for a, (code, scale) in enumerate(quantised(first, count, raw)):
                e, s = divmod(first + a, PASSES)
                if e < E - 1:
                    if s == 0:
                        acc = [psum.tile([P, N], F32, name="acc") for h in range(HALVES)]
                    for h in range(HALVES):
                        multiply(acc[h], e, s, h, code, scale)
                    if s == PASSES - 1:
                        waiting.append((e, acc))
                    if first + count >= SCALAR_PASSES:
                        for done in waiting:
                            finish(*done)
                        waiting.clear()
                    continue
                if s == 0:
                    acc = {(u, h): psum.tile([P, N // 2], F32, name="acc") for u in range(2) for h in range(HALVES)}
                for u in range(2):
                    cols = slice(u * N // 2, (u + 1) * N // 2)
                    for h in range(HALVES):
                        multiply(acc[u, h], e, s, h, code[:, cols], scale[:, cols])

        last = (E - 1) * HALVES
        positive = keep.tile([P, N], F32, name="positive")
        for u in range(2):
            cols = slice(u * N // 2, (u + 1) * N // 2)
            nc.scalar.activation(out=clipped[:, 0, cols], in_=acc[u, 0][:], func=ACT.Relu)
            nc.vector.tensor_scalar_max(positive[:, cols], acc[u, 1][:], 0.0)
            nc.scalar.activation(out=y[:, last, cols], in_=clipped[:, 0, cols], func=ACT.Square)
            nc.vector.tensor_tensor(y[:, last + 1, cols], positive[:, cols], positive[:, cols], mybir.AluOpType.mult)
        store(E - 1)
